import numpy as np, ml_dtypes
CORES = [88,96,104,112,120,216,224,232,240,248]
N = 10
T, G, CAP = 8192, 8192, 1024
def entries(a): return a.T.reshape(-1)
def pack(v, P): return np.ascontiguousarray(np.asarray(v, np.int32).reshape(-1, P).T)
def lists(rng, how):
    S = rng.integers(0, T, (N, 2 * CAP)); P = np.stack([rng.permutation(G)[:2 * CAP] for r in range(N)])
    if how == "alike": S[:] = rng.integers(0, T, (N, 1))
    if how == "edge":
        S = np.where(rng.random((N, 2 * CAP)) < 0.5, 0, T - 1); S[:, [0, CAP]] = 0; S[:, [1, CAP + 1]] = T - 1
        P[:, 1:-1] = np.stack([1 + rng.permutation(G - 2)[:2 * CAP - 2] for r in range(N)]); P[0::2, 0], P[0::2, -1] = 0, G - 1; P[1::2, 0], P[1::2, -1] = G - 1, 0
    if how == "mixed": P = np.stack([rng.permutation(2 * CAP) for r in range(N)]); P[1::2] += G - 2 * CAP
    if how == "sorted":
        S2, P2 = [-np.sort(-A.reshape(N, 2, CAP), axis=2).reshape(N, 2 * CAP) for A in (S, P)]; S, P = -np.sort(-S, axis=1), -np.sort(-P, axis=1)
        S[1::3], P[1::3] = S[1::3, ::-1].copy(), P[1::3, ::-1].copy(); S[2::3], P[2::3] = S2[2::3], P2[2::3]
    return {"snd": np.stack([pack(s, 16) for s in S]), "plc": np.stack([pack(q, 16) for q in P])}
def setup_inputs(rng):
    return dict({"x": rng.standard_normal((N, 128, T), dtype=np.float32).astype(ml_dtypes.bfloat16), "gh": rng.standard_normal((N, 128, G), dtype=np.float32).astype(ml_dtypes.bfloat16)}, **lists(rng, "uniform"))
def setup_inputs_alike(rng):
    d = setup_inputs(rng); d.update(lists(rng, "alike"))
    for k in ("x", "gh"): d[k] = (d[k].astype(np.float32) * 1048576.0).astype(d[k].dtype)
    return d
def setup_inputs_edge(rng):
    d = setup_inputs(rng); d.update(lists(rng, "edge"))
    for k in ("x", "gh"): d[k] = (d[k].astype(np.float32) * (1 / 1024.0)).astype(d[k].dtype)
    return d
def setup_inputs_mixed(rng):
    d = setup_inputs(rng); d.update(lists(rng, "mixed"))
    return d
def setup_inputs_sorted(rng):
    d = setup_inputs(rng); d.update(lists(rng, "sorted"))
    return d
def setup_inputs_zeros(rng):
    d = setup_inputs(rng); d.update(lists(rng, "zeros"))
    for r in range(N): d["x"][r][:, entries(d["snd"][r])[::2]] = 0
    return d
def check_inputs(x):
    bad = []
    if x["snd"].min() < 0 or x["snd"].max() >= T: bad.append("snd out of range")
    if x["plc"].min() < 0 or x["plc"].max() >= G: bad.append("plc out of range")
    if any(len(np.unique(a)) != a.size for a in x["plc"]): bad.append("a place is named twice")
    return bad
def reference(x, gh, snd, plc):
    y = gh.copy()
    for r in range(N):
        S = entries(snd[r]); lo, hi = (r - 1) % N, (r + 1) % N
        y[lo][:, entries(plc[lo])[CAP:]] = x[r][:, S[:CAP]]
        y[hi][:, entries(plc[hi])[:CAP]] = x[r][:, S[CAP:]]
    return {"y": y}

@@ -1,0 +1,251 @@
+from concourse.bass import DstId, RemoteDMATransfer
+from concourse.mybir import AluOpType, ActivationFunctionType
+
+ALL = 256
+G, CAP = 8192, 1024
+HALF = CAP // 2
+QW = G // 4
+DW = QW + 16 * 64 + 128
+GHA = 2048
+BLOCKS = [512, 1024, 1024, 1024, 512]
+NB = len(BLOCKS)
+
+SCRATCH = {
+    "xs": ("sbuf", [128, 8192], "bfloat16"),
+    "win": ("sbuf", [128, G + 2 * CAP], "bfloat16"),
+    "yb": ("sbuf", [128, G], "bfloat16"),
+    "sb": ("sbuf", [128, 2 * CAP], "bfloat16"),
+    "rb": ("sbuf", [128, HALF], "bfloat16"),
+    "li": ("sbuf", [128, 256], "int32"),
+    "lf": ("sbuf", [128, 256], "float32"),
+    "so": ("sbuf", [128, 128], "uint16"),
+    "ones": ("sbuf", [128, 128], "float32"),
+    "rep": ("sbuf", [128, 128], "float32"),
+    "sel": ("sbuf", [128, 144], "float32"),
+    "pcol": ("sbuf", [128, 1], "int32"),
+    "gri": ("sbuf", [128, 1], "int32"),
+    "pmi": ("sbuf", [128, 1], "int32"),
+    "grf": ("sbuf", [128, 1], "float32"),
+    "pmf": ("sbuf", [128, 1], "float32"),
+    "spare": ("sbuf", [128, 64], "int32"),
+    "pi": ("sbuf", [128, 64], "int32"),
+    "qi": ("sbuf", [128, 64], "int32"),
+    "ai": ("sbuf", [128, 64], "int32"),
+    "mine": ("sbuf", [128, 64], "float32"),
+    "ua": ("sbuf", [128, 64], "float32"),
+    "ub": ("sbuf", [128, 64], "float32"),
+    "uc": ("sbuf", [128, 64], "float32"),
+    "off": ("sbuf", [128, 64], "uint16"),
+    "vals": ("sbuf", [128, CAP], "float32"),
+    "wv": ("sbuf", [128, DW], "float32"),
+    "idb": ("sbuf", [128, 512], "float32"),
+    "idn": ("sbuf", [128, 512], "float32"),
+    "ot": ("sbuf", [128, 512], "float32"),
+    "inv": ("sbuf", [128, 512], "uint16"),
+    "pl": ("psum", [128, 512], "float32"),
+    "po": ("psum", [128, 512], "float32"),
+}
+SEMAPHORES = ["ld", "xl", "ghl", "st", "ones", "selz", "v", "rep", "pc", "vl", "vl2", "selr", "idr", "lfr", "plr", "sor",
+              "scr", "mo", "inr", "vg", "sg", "sent", "ls", "rin", "arr"] + \
+             ["yv%d" % k for k in range(NB)] + ["ys%d" % k for k in range(NB)]
+
+
+def bits(m):
+    return [e for e in range(16) if m >> e & 1]
+
+
+def maskof(es):
+    return sum(1 << e for e in es)
+
+
+def plan(rank, cores, topo):
+    n, me = len(cores), cores[rank]
+    chip = [c for c in range(ALL) if topo.host(c) == topo.host(me) and topo.chip(c) == topo.chip(me) and c != me]
+    used, out = [], []
+    for half, dst in ((0, cores[(rank - 1) % n]), (1, cores[(rank + 1) % n])):
+        relays = []
+        if not topo.may_write(me, dst):
+            free = [c for c in chip if topo.may_write(c, dst) and c not in used]
+            near = [c for c in free if topo.die(c) == topo.die(me)]
+            far = [c for c in free if topo.die(c) != topo.die(me)]
+            relays = [near[0], far[0]]
+            used += relays
+        out.append((half, dst, G + (CAP if half == 0 else 0), relays))
+    return out
+
+
+def rank_program(g, core, T, topo):
+    rank = T.rank_of(core)
+    cores = list(T.cores)
+    if rank is None:
+        relay(g, core, T, topo, cores)
+    else:
+        member(g, core, T, topo, cores, rank)
+
+
+def relay(g, core, T, topo, cores):
+    for r, me in enumerate(cores):
+        if topo.host(me) != topo.host(core) or topo.chip(me) != topo.chip(core):
+            continue
+        p = plan(r, cores, topo)
+        for half, dst, at, relays in p:
+            if core not in relays:
+                continue
+            k = relays.index(core)
+            rid, pid = topo.addr(dst, core)
+            m = topo.mask(core, dst)
+            g.wait_ge(T.sem.rin, len(relay_engines(me, p, topo)[core]))
+            a = at + k * HALF
+            g.remote_dma(T.win[:, a:a + HALF], T.rb[:], T.sem.arr, T.sem.ls, pid, rid, m)
+            g.wait_ge(T.sem.ls, len(bits(m)))
+
+
+def relay_engines(me, p, topo):
+    rel, taken = [], []
+    for half, dst, at, relays in p:
+        rel += relays
+        if not relays:
+            taken += bits(topo.mask(me, dst))
+    out = {}
+    for k, c in enumerate(rel):
+        es = [e for e in bits(topo.mask(me, c)) if e not in taken]
+        out[c] = es[k::len(rel)]
+    return out
+
+
+def arrivals(rank, cores, topo):
+    n, total = len(cores), 0
+    for s in ((rank - 1) % n, (rank + 1) % n):
+        for half, dst, at, relays in plan(s, cores, topo):
+            if dst == cores[rank]:
+                for c in (relays or [cores[s]]):
+                    total += len(bits(topo.mask(c, dst)))
+    return total
+
+
+def member(g, core, T, topo, cores, rank):
+    S = T.sem
+    V, A, PE, SY = g.vector, g.scalar, g.tensor, g.sync
+    p = plan(rank, cores, topo)
+    copy = ActivationFunctionType.Copy
+    n = [0]
+
+    def v(ins):
+        ins.then_inc(S.v, 1)
+        n[0] += 1
+
+    def vw():
+        V.wait_ge(S.v, n[0])
+
+    SY.dma_start(T.li[0:16, 0:128], T.snd[:]).then_inc(S.ld, 16)
+    A.dma_start(T.li[0:16, 128:256], T.plc[:]).then_inc(S.ld, 16)
+    SY.dma_start(T.xs[:], T.x[:]).then_inc(S.xl, 16)
+    SY.dma_start(T.win[:, 0:GHA], T.gh[:, 0:GHA]).then_inc(S.ghl, 16)
+    SY.wait_ge(S.sent, 1)
+    SY.dma_start(T.win[:, GHA:G], T.gh[:, GHA:G]).then_inc(S.ghl, 16)
+
+    g.wait_ge(S.ones, 1)
+    g.affine_select(T.rep[0:16, :], T.ones[0:16, :], [[0, 8], [-1, 16]], AluOpType.is_equal, 0.0, 0, 1).then_inc(S.rep, 1)
+    g.iota(T.pcol[:], [[0, 1]], 0, 1).then_inc(S.pc, 1)
+    g.iota(T.spare[:], [[16, 64]], QW, 1).then_inc(S.pc, 1)
+    g.iota(T.vals[:], [[1, CAP]], G, 0, allow_small_or_imprecise_dtypes=True).then_inc(S.vl, 1)
+    g.wait_ge(S.selz, 1)
+    g.affine_select(T.sel[:], T.sel[:], [[0, 9], [1024, 4], [-16, 4]], AluOpType.not_equal, 1.0, -3 * 1024, 1).then_inc(S.selr, 1)
+    g.wait_ge(S.selr, 1)
+    g.affine_select(T.sel[:], T.sel[:], [[0, 9], [1024, 4], [-16, 4]], AluOpType.not_equal, 1.0, -3 * 1024 - 64, 1).then_inc(S.selr, 1)
+    g.iota(T.idb[:], [[16, 512]], 0, 0, allow_small_or_imprecise_dtypes=True).then_inc(S.idr, 1)
+
+    V.memset(T.ones[0:16, :], 1.0).then_inc(S.ones, 1)
+    V.memset(T.sel[:], 0.0).then_inc(S.selz, 1)
+    v(V.memset(T.wv[:, 0:QW], 0.0))
+    V.wait_ge(S.pc, 2)
+    v(V.tensor_scalar(T.gri[:], T.pcol[:], 4, 3, AluOpType.logical_shift_right, AluOpType.bitwise_and))
+    v(V.tensor_scalar(T.pmi[:], T.pcol[:], 15, None, AluOpType.bitwise_and))
+    vw()
+    v(V.tensor_copy(T.grf[:], T.gri[:]))
+    v(V.tensor_copy(T.pmf[:], T.pmi[:]))
+    V.wait_ge(S.ld, 32)
+    V.tensor_copy(T.lf[0:16, :], T.li[0:16, :]).then_inc(S.lfr, 1)
+    PE.wait_ge(S.rep, 1)
+    PE.wait_ge(S.lfr, 1)
+    PE.matmul(T.pl[:, 0:256], T.rep[0:16, :], T.lf[0:16, :], True, True).then_inc(S.plr, 1)
+    V.wait_ge(S.plr, 1)
+    V.tensor_copy(T.so[:], T.pl[:, 0:128]).then_inc(S.sor, 1)
+    v(V.tensor_copy(T.pi[0:64, :], T.pl[0:64, 128:192]))
+    v(V.tensor_copy(T.pi[64:128, :], T.pl[64:128, 192:256]))
+    vw()
+    v(V.tensor_scalar(T.qi[:], T.pi[:], 2, None, AluOpType.logical_shift_right))
+    v(V.tensor_scalar(T.ai[:], T.pi[:], 3, None, AluOpType.bitwise_and))
+    vw()
+    v(V.tensor_tensor(T.ua[:], T.qi[:], T.spare[:], AluOpType.subtract))
+    v(V.tensor_scalar(T.mine[:], T.ai[:], T.grf[:], None, AluOpType.is_equal))
+    vw()
+    v(V.tensor_tensor(T.ub[:], T.ua[:], T.mine[:], AluOpType.mult))
+    vw()
+    v(V.tensor_tensor(T.uc[:], T.ub[:], T.spare[:], AluOpType.add))
+    vw()
+    v(V.tensor_copy(T.off[:], T.uc[:]))
+    vw()
+    V.wait_ge(S.vl2, 1)
+    V.tensor_copy(T.wv[:, 0:DW].indirect(T.off[:, 0:64]), T.vals[:]).then_inc(S.scr, 1)
+
+    A.wait_ge(S.vl, 1)
+    A.activation(T.vals[64:128, :], T.vals[64:128, :], copy, bias=float(CAP)).then_inc(S.vl2, 1)
+    V.wait_ge(S.xl, 16)
+    V.wait_ge(S.sor, 1)
+    V.tensor_copy(T.sb[:, 0:CAP], T.xs[:, 0:8192].indirect(T.so[:, 0:64])).then_inc(S.vg, 1)
+    A.wait_ge(S.xl, 16)
+    A.wait_ge(S.sor, 1)
+    A.activation(T.sb[:, CAP:2 * CAP], T.xs[:, 0:8192].indirect(T.so[:, 64:128]), copy, bias=-0.0).then_inc(S.sg, 1)
+
+    g.wait_ge(S.vg, 1)
+    g.wait_ge(S.sg, 1)
+    eng = relay_engines(core, p, topo)
+    left, trs = 0, []
+    for half, dst, at, relays in p:
+        for k, c in enumerate(relays):
+            rid, pid = topo.addr(c, core)
+            a = half * CAP + k * HALF
+            trs.append(RemoteDMATransfer(dst_ids=[DstId(rid=rid, pnc=pid)], dma_engine_mask=maskof(eng[c]), remote_sem=S.rin,
+                                         src=T.sb[:, a:a + HALF], dst=T.rb[:]))
+            left += len(eng[c])
+    if trs:
+        g.remote_dma_fused(trs, local_sem=S.ls)
+    for half, dst, at, relays in p:
+        if not relays:
+            rid, pid = topo.addr(dst, core)
+            m = topo.mask(core, dst)
+            g.remote_dma(T.win[:, at:at + CAP], T.sb[:, half * CAP:(half + 1) * CAP], S.arr, S.ls, pid, rid, m)
+            left += len(bits(m))
+    g.sem_inc(S.sent, 1)
+    g.wait_ge(S.ls, left)
+
+    PE.wait_ge(S.selr, 2)
+    PE.wait_ge(S.scr, 1)
+    for h in range(4):
+        ins = PE.matmul(T.po[:], T.sel[:, 12 - 4 * h:140 - 4 * h], T.wv[:, h:QW:4], h == 0, h == 3)
+    ins.then_inc(S.mo, 1)
+    V.wait_ge(S.idr, 1)
+    v(V.tensor_scalar(T.idn[:], T.idb[:], T.pmf[:], None, AluOpType.add))
+    vw()
+    V.wait_ge(S.mo, 1)
+    v(V.tensor_tensor(T.ot[:], T.po[:], T.idn[:], AluOpType.max))
+    vw()
+    V.tensor_copy(T.inv[:], T.ot[:]).then_inc(S.inr, 1)
+
+    total = arrivals(rank, cores, topo)
+    for q in (V, A):
+        q.wait_ge(S.inr, 1)
+        q.wait_ge(S.ghl, 32)
+        q.wait_ge(S.arr, total)
+    at = 0
+    for k, w in enumerate(BLOCKS):
+        a, b, c = at, at + w, at + 2 * w
+        V.tensor_copy(T.yb[:, a:b], T.win[:].indirect(T.inv[:, a // 16:b // 16])).then_inc(S["yv%d" % k], 1)
+        A.activation(T.yb[:, b:c], T.win[:].indirect(T.inv[:, b // 16:c // 16]), copy, bias=-0.0).then_inc(S["ys%d" % k], 1)
+        SY.wait_ge(S["yv%d" % k], 1)
+        SY.dma_start(T.y[:, a:b], T.yb[:, a:b]).then_inc(S.st, 16)
+        SY.wait_ge(S["ys%d" % k], 1)
+        SY.dma_start(T.y[:, b:c], T.yb[:, b:c]).then_inc(S.st, 16)
+        at = c
+    SY.wait_ge(S.st, 2 * NB * 16)

@@ -6,6 +6,7 @@ G, CAP = 8192, 1024
 HALF = CAP // 2
 QW = G // 4
 DW = QW + 16 * 64 + 128
+NONE = 8192
 GHA = 2048
 BLOCKS = [512, 1024, 1024, 1024, 512]
 NB = len(BLOCKS)
@@ -22,6 +23,7 @@ SCRATCH = {
     "ones": ("sbuf", [128, 128], "float32"),
     "rep": ("sbuf", [128, 128], "float32"),
     "sel": ("sbuf", [128, 144], "float32"),
+    "selh": ("sbuf", [128, 144], "float16"),
     "pcol": ("sbuf", [128, 1], "int32"),
     "gri": ("sbuf", [128, 1], "int32"),
     "pmi": ("sbuf", [128, 1], "int32"),
@@ -38,15 +40,18 @@ SCRATCH = {
     "off": ("sbuf", [128, 64], "uint16"),
     "vals": ("sbuf", [128, CAP], "float32"),
     "wv": ("sbuf", [128, DW], "float32"),
+    "wh": ("sbuf", [128, QW], "float16"),
     "idb": ("sbuf", [128, 512], "float32"),
     "idn": ("sbuf", [128, 512], "float32"),
     "ot": ("sbuf", [128, 512], "float32"),
     "inv": ("sbuf", [128, 512], "uint16"),
-    "pl": ("psum", [128, 512], "float32"),
+    "plp": ("psum", [128, 512], "float32"),
+    "pls": ("psum", [128, 512], "float32"),
     "po": ("psum", [128, 512], "float32"),
 }
-SEMAPHORES = ["ld", "xl", "ghl", "st", "ones", "selz", "v", "rep", "pc", "vl", "vl2", "selr", "idr", "lfr", "plr", "sor",
-              "scr", "mo", "inr", "vg", "sg", "sent", "ls", "rin", "arr"] + \
+SEMAPHORES = ["ldp", "lds", "xl", "ghl", "st", "ones", "selz", "v", "rep", "pc", "vl", "vl2", "selr", "selc", "idr", "lfp",
+              "lfs", "plpr", "plsr", "sor", "scr", "scs", "mo", "inr", "vg0", "vg1", "sg0", "sg1", "sent", "ls", "rin", "arr",
+              "cv0", "cv1", "cv2", "cv3"] + \
              ["yv%d" % k for k in range(NB)] + ["ys%d" % k for k in range(NB)]
 
 
@@ -68,10 +73,35 @@ def plan(rank, cores, topo):
             free = [c for c in chip if topo.may_write(c, dst) and c not in used]
             near = [c for c in free if topo.die(c) == topo.die(me)]
             far = [c for c in free if topo.die(c) != topo.die(me)]
-            relays = [near[0], far[0]]
+            relays = [far[0], near[0]] if used else [near[0], far[0]]
             used += relays
         out.append((half, dst, G + (CAP if half == 0 else 0), relays))
     return out
+
+
+def relay_engines(me, p, topo):
+    taken = []
+    for half, dst, at, relays in p:
+        if not relays:
+            taken += bits(topo.mask(me, dst))
+    out = {}
+    rel = [relays for half, dst, at, relays in p if relays]
+    for step in (0, 1):
+        cs = sorted([relays[step] for relays in rel], key=lambda c: topo.die(c) != topo.die(me))
+        for k, c in enumerate(cs):
+            es = [e for e in bits(topo.mask(me, c)) if e not in taken]
+            out[c] = es[k::len(cs)]
+    return out
+
+
+def arrivals(rank, cores, topo):
+    n, total = len(cores), 0
+    for s in ((rank - 1) % n, (rank + 1) % n):
+        for half, dst, at, relays in plan(s, cores, topo):
+            if dst == cores[rank]:
+                for c in (relays or [cores[s]]):
+                    total += len(bits(topo.mask(c, dst)))
+    return total
 
 
 def rank_program(g, core, T, topo):
@@ -91,36 +121,12 @@ def relay(g, core, T, topo, cores):
         for half, dst, at, relays in p:
             if core not in relays:
                 continue
-            k = relays.index(core)
             rid, pid = topo.addr(dst, core)
             m = topo.mask(core, dst)
+            a = at + relays.index(core) * HALF
             g.wait_ge(T.sem.rin, len(relay_engines(me, p, topo)[core]))
-            a = at + k * HALF
             g.remote_dma(T.win[:, a:a + HALF], T.rb[:], T.sem.arr, T.sem.ls, pid, rid, m)
             g.wait_ge(T.sem.ls, len(bits(m)))
-
-
-def relay_engines(me, p, topo):
-    rel, taken = [], []
-    for half, dst, at, relays in p:
-        rel += relays
-        if not relays:
-            taken += bits(topo.mask(me, dst))
-    out = {}
-    for k, c in enumerate(rel):
-        es = [e for e in bits(topo.mask(me, c)) if e not in taken]
-        out[c] = es[k::len(rel)]
-    return out
-
-
-def arrivals(rank, cores, topo):
-    n, total = len(cores), 0
-    for s in ((rank - 1) % n, (rank + 1) % n):
-        for half, dst, at, relays in plan(s, cores, topo):
-            if dst == cores[rank]:
-                for c in (relays or [cores[s]]):
-                    total += len(bits(topo.mask(c, dst)))
-    return total
 
 
 def member(g, core, T, topo, cores, rank):
@@ -137,8 +143,8 @@ def member(g, core, T, topo, cores, rank):
     def vw():
         V.wait_ge(S.v, n[0])
 
-    SY.dma_start(T.li[0:16, 0:128], T.snd[:]).then_inc(S.ld, 16)
-    A.dma_start(T.li[0:16, 128:256], T.plc[:]).then_inc(S.ld, 16)
+    A.dma_start(T.li[0:16, 128:256], T.plc[:]).then_inc(S.ldp, 16)
+    SY.dma_start(T.li[0:16, 0:128], T.snd[:]).then_inc(S.lds, 16)
     SY.dma_start(T.xs[:], T.x[:]).then_inc(S.xl, 16)
     SY.dma_start(T.win[:, 0:GHA], T.gh[:, 0:GHA]).then_inc(S.ghl, 16)
     SY.wait_ge(S.sent, 1)
@@ -148,31 +154,34 @@ def member(g, core, T, topo, cores, rank):
     g.affine_select(T.rep[0:16, :], T.ones[0:16, :], [[0, 8], [-1, 16]], AluOpType.is_equal, 0.0, 0, 1).then_inc(S.rep, 1)
     g.iota(T.pcol[:], [[0, 1]], 0, 1).then_inc(S.pc, 1)
     g.iota(T.spare[:], [[16, 64]], QW, 1).then_inc(S.pc, 1)
-    g.iota(T.vals[:], [[1, CAP]], G, 0, allow_small_or_imprecise_dtypes=True).then_inc(S.vl, 1)
+    g.iota(T.vals[:], [[1, CAP]], 0, 0, allow_small_or_imprecise_dtypes=True).then_inc(S.vl, 1)
     g.wait_ge(S.selz, 1)
     g.affine_select(T.sel[:], T.sel[:], [[0, 9], [1024, 4], [-16, 4]], AluOpType.not_equal, 1.0, -3 * 1024, 1).then_inc(S.selr, 1)
     g.wait_ge(S.selr, 1)
     g.affine_select(T.sel[:], T.sel[:], [[0, 9], [1024, 4], [-16, 4]], AluOpType.not_equal, 1.0, -3 * 1024 - 64, 1).then_inc(S.selr, 1)
-    g.iota(T.idb[:], [[16, 512]], 0, 0, allow_small_or_imprecise_dtypes=True).then_inc(S.idr, 1)
+    g.iota(T.idb[:], [[16, 512]], -2 * NONE, 0, allow_small_or_imprecise_dtypes=True).then_inc(S.idr, 1)
 
     V.memset(T.ones[0:16, :], 1.0).then_inc(S.ones, 1)
     V.memset(T.sel[:], 0.0).then_inc(S.selz, 1)
-    v(V.memset(T.wv[:, 0:QW], 0.0))
+    v(V.memset(T.wv[:, 0:QW], -float(NONE)))
     V.wait_ge(S.pc, 2)
     v(V.tensor_scalar(T.gri[:], T.pcol[:], 4, 3, AluOpType.logical_shift_right, AluOpType.bitwise_and))
     v(V.tensor_scalar(T.pmi[:], T.pcol[:], 15, None, AluOpType.bitwise_and))
     vw()
     v(V.tensor_copy(T.grf[:], T.gri[:]))
     v(V.tensor_copy(T.pmf[:], T.pmi[:]))
-    V.wait_ge(S.ld, 32)
-    V.tensor_copy(T.lf[0:16, :], T.li[0:16, :]).then_inc(S.lfr, 1)
+    V.wait_ge(S.ldp, 16)
+    V.tensor_copy(T.lf[0:16, 128:256], T.li[0:16, 128:256]).then_inc(S.lfp, 1)
+    V.wait_ge(S.lds, 16)
+    V.tensor_copy(T.lf[0:16, 0:128], T.li[0:16, 0:128]).then_inc(S.lfs, 1)
     PE.wait_ge(S.rep, 1)
-    PE.wait_ge(S.lfr, 1)
-    PE.matmul(T.pl[:, 0:256], T.rep[0:16, :], T.lf[0:16, :], True, True).then_inc(S.plr, 1)
-    V.wait_ge(S.plr, 1)
-    V.tensor_copy(T.so[:], T.pl[:, 0:128]).then_inc(S.sor, 1)
-    v(V.tensor_copy(T.pi[0:64, :], T.pl[0:64, 128:192]))
-    v(V.tensor_copy(T.pi[64:128, :], T.pl[64:128, 192:256]))
+    PE.wait_ge(S.lfp, 1)
+    PE.matmul(T.plp[:, 0:128], T.rep[0:16, :], T.lf[0:16, 128:256], True, True).then_inc(S.plpr, 1)
+    PE.wait_ge(S.lfs, 1)
+    PE.matmul(T.pls[:, 0:128], T.rep[0:16, :], T.lf[0:16, 0:128], True, True).then_inc(S.plsr, 1)
+    V.wait_ge(S.plpr, 1)
+    v(V.tensor_copy(T.pi[0:64, :], T.plp[0:64, 0:64]))
+    v(V.tensor_copy(T.pi[64:128, :], T.plp[64:128, 64:128]))
     vw()
     v(V.tensor_scalar(T.qi[:], T.pi[:], 2, None, AluOpType.logical_shift_right))
     v(V.tensor_scalar(T.ai[:], T.pi[:], 3, None, AluOpType.bitwise_and))
@@ -186,31 +195,40 @@ def member(g, core, T, topo, cores, rank):
     vw()
     v(V.tensor_copy(T.off[:], T.uc[:]))
     vw()
-    V.wait_ge(S.vl2, 1)
-    V.tensor_copy(T.wv[:, 0:DW].indirect(T.off[:, 0:64]), T.vals[:]).then_inc(S.scr, 1)
-
     A.wait_ge(S.vl, 1)
     A.activation(T.vals[64:128, :], T.vals[64:128, :], copy, bias=float(CAP)).then_inc(S.vl2, 1)
-    V.wait_ge(S.xl, 16)
-    V.wait_ge(S.sor, 1)
-    V.tensor_copy(T.sb[:, 0:CAP], T.xs[:, 0:8192].indirect(T.so[:, 0:64])).then_inc(S.vg, 1)
-    A.wait_ge(S.xl, 16)
-    A.wait_ge(S.sor, 1)
-    A.activation(T.sb[:, CAP:2 * CAP], T.xs[:, 0:8192].indirect(T.so[:, 64:128]), copy, bias=-0.0).then_inc(S.sg, 1)
+    V.wait_ge(S.vl2, 1)
+    V.tensor_copy(T.wv[:, 0:DW].indirect(T.off[:, 0:32]), T.vals[:, 0:512]).then_inc(S.scr, 1)
+    V.wait_ge(S.plsr, 1)
+    V.tensor_copy(T.so[:], T.pls[:, 0:128]).then_inc(S.sor, 1)
+    V.wait_ge(S.selr, 2)
+    V.tensor_copy(T.selh[:], T.sel[:]).then_inc(S.selc, 1)
 
-    g.wait_ge(S.vg, 1)
-    g.wait_ge(S.sg, 1)
+    for q in (V, A):
+        q.wait_ge(S.xl, 16)
+        q.wait_ge(S.sor, 1)
+    for k in (0, 1):
+        a, b, c = k * HALF, k * HALF + HALF, CAP + k * HALF
+        V.tensor_copy(T.sb[:, a:b], T.xs[:].indirect(T.so[:, a // 16:b // 16])).then_inc(S["vg%d" % k], 1)
+        A.activation(T.sb[:, c:c + HALF], T.xs[:].indirect(T.so[:, c // 16:(c + HALF) // 16]), copy,
+                     bias=-0.0).then_inc(S["sg%d" % k], 1)
+
     eng = relay_engines(core, p, topo)
-    left, trs = 0, []
-    for half, dst, at, relays in p:
-        for k, c in enumerate(relays):
-            rid, pid = topo.addr(c, core)
-            a = half * CAP + k * HALF
-            trs.append(RemoteDMATransfer(dst_ids=[DstId(rid=rid, pnc=pid)], dma_engine_mask=maskof(eng[c]), remote_sem=S.rin,
-                                         src=T.sb[:, a:a + HALF], dst=T.rb[:]))
-            left += len(eng[c])
-    if trs:
-        g.remote_dma_fused(trs, local_sem=S.ls)
+    left = 0
+    for k in (0, 1):
+        g.wait_ge(S["vg%d" % k], 1)
+        g.wait_ge(S["sg%d" % k], 1)
+        trs = []
+        for half, dst, at, relays in p:
+            if relays:
+                c = relays[k]
+                rid, pid = topo.addr(c, core)
+                a = half * CAP + k * HALF
+                trs.append(RemoteDMATransfer(dst_ids=[DstId(rid=rid, pnc=pid)], dma_engine_mask=maskof(eng[c]),
+                                             remote_sem=S.rin, src=T.sb[:, a:a + HALF], dst=T.rb[:]))
+                left += len(eng[c])
+        if trs:
+            g.remote_dma_fused(trs, local_sem=S.ls)
     for half, dst, at, relays in p:
         if not relays:
             rid, pid = topo.addr(dst, core)
@@ -220,10 +238,14 @@ def member(g, core, T, topo, cores, rank):
     g.sem_inc(S.sent, 1)
     g.wait_ge(S.ls, left)
 
-    PE.wait_ge(S.selr, 2)
-    PE.wait_ge(S.scr, 1)
+    V.wait_ge(S.scr, 1)
+    V.tensor_copy(T.wv[:, 0:DW].indirect(T.off[:, 32:64]), T.vals[:, 512:CAP]).then_inc(S.scs, 1)
+    V.wait_ge(S.scs, 1)
+    PE.wait_ge(S.selc, 1)
     for h in range(4):
-        ins = PE.matmul(T.po[:], T.sel[:, 12 - 4 * h:140 - 4 * h], T.wv[:, h:QW:4], h == 0, h == 3)
+        V.tensor_copy(T.wh[:, 512 * h:512 * h + 512], T.wv[:, h:QW:4]).then_inc(S["cv%d" % h], 1)
+        PE.wait_ge(S["cv%d" % h], 1)
+        ins = PE.matmul(T.po[:], T.selh[:, 12 - 4 * h:140 - 4 * h], T.wh[:, 512 * h:512 * h + 512], h == 0, h == 3)
     ins.then_inc(S.mo, 1)
     V.wait_ge(S.idr, 1)
     v(V.tensor_scalar(T.idn[:], T.idb[:], T.pmf[:], None, AluOpType.add))
@@ -231,7 +253,7 @@ def member(g, core, T, topo, cores, rank):
     V.wait_ge(S.mo, 1)
     v(V.tensor_tensor(T.ot[:], T.po[:], T.idn[:], AluOpType.max))
     vw()
-    V.tensor_copy(T.inv[:], T.ot[:]).then_inc(S.inr, 1)
+    V.tensor_scalar(T.inv[:], T.ot[:], float(2 * NONE), None, AluOpType.add).then_inc(S.inr, 1)
 
     total = arrivals(rank, cores, topo)
     for q in (V, A):

@@ -3,44 +3,45 @@ from concourse.mybir import AluOpType, ActivationFunctionType
 
 ALL = 256
 G, CAP = 8192, 1024
-HALF = CAP // 2
-QW = G // 4
-DW = QW + 16 * 64 + 128
+STEP = [0, 608, 1024]
+ENT = 2 * CAP // 4
+QW = G // 2
+DW = QW + ENT + 128
+WV = 3072
 NONE = 8192
-GHA = 2048
-BLOCKS = [512, 1024, 1024, 1024, 512]
+BASE = 4 * NONE
+GHP = [0, 3072, 5632, 8192]
+BLOCKS = [384, 704, 1024, 960, 640, 384]
 NB = len(BLOCKS)
+CH = (G - 2 * BLOCKS[-1]) // 16
+
+COLI = ["pcol", "pm", "gr", "e5", "a30"]
+COLF = ["grf", "pmf", "cs0", "cs1", "c0", "c1", "ef", "be0", "be1"]
 
 SCRATCH = {
     "xs": ("sbuf", [128, 8192], "bfloat16"),
     "win": ("sbuf", [128, G + 2 * CAP], "bfloat16"),
     "yb": ("sbuf", [128, G], "bfloat16"),
     "sb": ("sbuf", [128, 2 * CAP], "bfloat16"),
-    "rb": ("sbuf", [128, HALF], "bfloat16"),
+    "rb": ("sbuf", [128, STEP[1]], "bfloat16"),
     "li": ("sbuf", [128, 256], "int32"),
     "lf": ("sbuf", [128, 256], "float32"),
     "so": ("sbuf", [128, 128], "uint16"),
     "ones": ("sbuf", [128, 128], "float32"),
     "rep": ("sbuf", [128, 128], "float32"),
-    "sel": ("sbuf", [128, 144], "float32"),
-    "selh": ("sbuf", [128, 144], "float16"),
-    "pcol": ("sbuf", [128, 1], "int32"),
-    "gri": ("sbuf", [128, 1], "int32"),
-    "pmi": ("sbuf", [128, 1], "int32"),
-    "grf": ("sbuf", [128, 1], "float32"),
-    "pmf": ("sbuf", [128, 1], "float32"),
-    "spare": ("sbuf", [128, 64], "int32"),
-    "pi": ("sbuf", [128, 64], "int32"),
-    "qi": ("sbuf", [128, 64], "int32"),
-    "ai": ("sbuf", [128, 64], "int32"),
-    "mine": ("sbuf", [128, 64], "float32"),
-    "ua": ("sbuf", [128, 64], "float32"),
-    "ub": ("sbuf", [128, 64], "float32"),
-    "uc": ("sbuf", [128, 64], "float32"),
-    "off": ("sbuf", [128, 64], "uint16"),
-    "vals": ("sbuf", [128, CAP], "float32"),
-    "wv": ("sbuf", [128, DW], "float32"),
-    "wh": ("sbuf", [128, QW], "float16"),
+    "sel": ("sbuf", [128, 144], "bfloat16"),
+    "spare": ("sbuf", [128, 32], "int32"),
+    "pi": ("sbuf", [128, 32], "int32"),
+    "qi": ("sbuf", [128, 32], "int32"),
+    "ai": ("sbuf", [128, 32], "int32"),
+    "mine": ("sbuf", [128, 32], "float32"),
+    "ua": ("sbuf", [128, 32], "float32"),
+    "ub": ("sbuf", [128, 32], "float32"),
+    "uc": ("sbuf", [128, 32], "float32"),
+    "off": ("sbuf", [128, 32], "uint16"),
+    "lo": ("sbuf", [128, 256], "float32"),
+    "vals": ("sbuf", [128, ENT], "bfloat16"),
+    "wv": ("sbuf", [128, DW], "bfloat16"),
     "idb": ("sbuf", [128, 512], "float32"),
     "idn": ("sbuf", [128, 512], "float32"),
     "ot": ("sbuf", [128, 512], "float32"),
@@ -49,10 +50,11 @@ SCRATCH = {
     "pls": ("psum", [128, 512], "float32"),
     "po": ("psum", [128, 512], "float32"),
 }
-SEMAPHORES = ["ldp", "lds", "xl", "ghl", "st", "ones", "selz", "v", "rep", "pc", "vl", "vl2", "selr", "selc", "idr", "lfp",
-              "lfs", "plpr", "plsr", "sor", "scr", "scs", "mo", "inr", "vg0", "vg1", "sg0", "sg1", "sent", "ls", "rin", "arr",
-              "cv0", "cv1", "cv2", "cv3"] + \
-             ["yv%d" % k for k in range(NB)] + ["ys%d" % k for k in range(NB)]
+SCRATCH.update({k: ("sbuf", [128, 1], "int32") for k in COLI})
+SCRATCH.update({k: ("sbuf", [128, 1], "float32") for k in COLF})
+SEMAPHORES = ["ldp", "lds", "xl", "ghl", "st", "ones", "v", "rep", "pc", "lor", "wvr", "sell", "selr", "idr", "idl", "idnr", "lfp",
+              "lfs", "plpr", "plsr", "pir", "pia", "sor", "scr", "mo", "inr", "invh", "vg0", "vg1", "sg0", "sg1", "sent0", "sent1",
+              "ls", "rin", "arr"] + ["yv%d" % k for k in range(NB)] + ["ys%d" % k for k in range(NB)]
 
 
 def bits(m):
@@ -63,20 +65,35 @@ def maskof(es):
     return sum(1 << e for e in es)
 
 
+def chip_of(me, topo):
+    return [c for c in range(ALL) if topo.host(c) == topo.host(me) and topo.chip(c) == topo.chip(me) and c != me]
+
+
 def plan(rank, cores, topo):
     n, me = len(cores), cores[rank]
-    chip = [c for c in range(ALL) if topo.host(c) == topo.host(me) and topo.chip(c) == topo.chip(me) and c != me]
     used, out = [], []
     for half, dst in ((0, cores[(rank - 1) % n]), (1, cores[(rank + 1) % n])):
         relays = []
         if not topo.may_write(me, dst):
-            free = [c for c in chip if topo.may_write(c, dst) and c not in used]
+            free = [c for c in chip_of(me, topo) if topo.may_write(c, dst) and c not in used]
             near = [c for c in free if topo.die(c) == topo.die(me)]
             far = [c for c in free if topo.die(c) != topo.die(me)]
             relays = [far[0], near[0]] if used else [near[0], far[0]]
             used += relays
         out.append((half, dst, G + (CAP if half == 0 else 0), relays))
     return out
+
+
+def relays_of(p):
+    return [c for half, dst, at, relays in p for c in relays]
+
+
+def helper_of(me, p, topo):
+    return [c for c in chip_of(me, topo) if topo.die(c) == topo.die(me) and c not in relays_of(p)][0]
+
+
+def helper_mask(helper, me, topo):
+    return maskof(bits(topo.mask(helper, me))[::2])
 
 
 def relay_engines(me, p, topo):
@@ -99,175 +116,279 @@ def arrivals(rank, cores, topo):
     for s in ((rank - 1) % n, (rank + 1) % n):
         for half, dst, at, relays in plan(s, cores, topo):
             if dst == cores[rank]:
-                for c in (relays or [cores[s]]):
+                for c in (relays or [cores[s]] * 2):
                     total += len(bits(topo.mask(c, dst)))
     return total
+
+
+def table_part(k, n):
+    return CH * k // n // 4 * 4, CH * (k + 1) // n // 4 * 4
 
 
 def rank_program(g, core, T, topo):
     rank = T.rank_of(core)
     cores = list(T.cores)
-    if rank is None:
-        relay(g, core, T, topo, cores)
-    else:
+    if rank is not None:
         member(g, core, T, topo, cores, rank)
-
-
-def relay(g, core, T, topo, cores):
+        return
     for r, me in enumerate(cores):
-        if topo.host(me) != topo.host(core) or topo.chip(me) != topo.chip(core):
-            continue
-        p = plan(r, cores, topo)
-        for half, dst, at, relays in p:
-            if core not in relays:
-                continue
-            rid, pid = topo.addr(dst, core)
-            m = topo.mask(core, dst)
-            a = at + relays.index(core) * HALF
-            g.wait_ge(T.sem.rin, len(relay_engines(me, p, topo)[core]))
-            g.remote_dma(T.win[:, a:a + HALF], T.rb[:], T.sem.arr, T.sem.ls, pid, rid, m)
-            g.wait_ge(T.sem.ls, len(bits(m)))
+        if core in chip_of(me, topo):
+            p = plan(r, cores, topo)
+            if core in relays_of(p):
+                relay(g, core, T, topo, me, p)
+            elif core == helper_of(me, p, topo):
+                helper(g, core, T, topo, me)
+
+
+def vector_chain(T, V):
+    n = [0]
+
+    def v(*ins):
+        for i in ins:
+            i.then_inc(T.sem.v, 1)
+            n[0] += 1
+
+    def vw():
+        V.wait_ge(T.sem.v, n[0])
+    return v, vw
+
+
+def make_table(g, T, v, vw, a, b):
+    V = g.vector
+    v(V.tensor_copy(T.pmf[:], T.pm[:]))
+    vw()
+    V.wait_ge(T.sem.idr, 1)
+    V.tensor_scalar(T.idn[:, a:b], T.idb[:, a:b], T.pmf[:], None, AluOpType.add).then_inc(T.sem.idl, 1)
+
+
+def relay(g, core, T, topo, me, p):
+    S, V = T.sem, g.vector
+    v, vw = vector_chain(T, V)
+    rel = relays_of(p)
+    half, dst, at, relays = [q for q in p if core in q[3]][0]
+    m = topo.mask(core, dst)
+    a, b = table_part(rel.index(core), len(rel))
+    g.iota(T.pcol[:], [[0, 1]], 0, 1).then_inc(S.pc, 1)
+    g.iota(T.idb[:, a:b], [[16, b - a]], 16 * a - BASE, 0, allow_small_or_imprecise_dtypes=True).then_inc(S.idr, 1)
+    V.wait_ge(S.pc, 1)
+    v(V.tensor_scalar(T.pm[:], T.pcol[:], 15, None, AluOpType.bitwise_and))
+    vw()
+    make_table(g, T, v, vw, a, b)
+    g.wait_ge(S.idl, 1)
+    rid, pid = topo.addr(me, core)
+    g.remote_dma(T.idn[:, a:b], T.idn[:, a:b], S.idnr, S.ls, pid, rid, m)
+    rid, pid = topo.addr(dst, core)
+    k = relays.index(core)
+    g.wait_ge(S.rin, len(relay_engines(me, p, topo)[core]))
+    g.remote_dma(T.win[:, at + STEP[k]:at + STEP[k + 1]], T.rb[:, 0:STEP[k + 1] - STEP[k]], S.arr, S.ls, pid, rid, m)
+    g.wait_ge(S.ls, 2 * len(bits(m)))
+
+
+def columns(g, T, v, vw):
+    S, V = T.sem, g.vector
+    ts = V.tensor_scalar
+    v(V.memset(T.wv[:, 0:WV], -float(NONE // 2)))
+    V.wait_ge(S.pc, 2)
+    v(ts(T.pm[:], T.pcol[:], 15, None, AluOpType.bitwise_and),
+      ts(T.e5[:], T.pcol[:], 5, None, AluOpType.logical_shift_right),
+      ts(T.gr[:], T.pcol[:], 4, 1, AluOpType.logical_shift_right, AluOpType.bitwise_and))
+    vw()
+    v(V.tensor_copy(T.grf[:], T.gr[:]),
+      ts(T.cs0[:], T.pm[:], 0.0, None, AluOpType.is_equal),
+      ts(T.cs1[:], T.pm[:], 1.0, None, AluOpType.is_equal),
+      ts(T.ef[:], T.e5[:], float(ENT), None, AluOpType.mult))
+    vw()
+
+
+def numbers(g, T, v, vw):
+    S, V = T.sem, g.vector
+    ts = V.tensor_scalar
+    v(V.tensor_tensor(T.be0[:], T.ef[:], T.cs0[:], AluOpType.mult))
+    vw()
+    v(ts(T.be1[:], T.cs0[:], 256.0, T.be0[:], AluOpType.mult, AluOpType.add))
+    vw()
+    V.wait_ge(S.lor, 1)
+    v(ts(T.vals[:, 0:256], T.lo[:], T.cs1[:], T.be0[:], AluOpType.mult, AluOpType.add),
+      ts(T.vals[:, 256:512], T.lo[:], T.cs1[:], T.be1[:], AluOpType.mult, AluOpType.add))
+
+
+def offsets(g, T, v, vw):
+    V = g.vector
+    ts, tt = V.tensor_scalar, V.tensor_tensor
+    v(ts(T.qi[:], T.pi[:], 1, None, AluOpType.logical_shift_right),
+      ts(T.ai[:], T.pi[:], 1, None, AluOpType.bitwise_and))
+    vw()
+    v(tt(T.ua[:], T.qi[:], T.spare[:], AluOpType.subtract),
+      ts(T.mine[:], T.ai[:], T.grf[:], None, AluOpType.is_equal))
+    vw()
+    v(tt(T.ub[:], T.ua[:], T.mine[:], AluOpType.mult))
+    vw()
+    v(tt(T.uc[:], T.ub[:], T.spare[:], AluOpType.add))
+    vw()
+    v(V.tensor_copy(T.off[:], T.uc[:]))
+
+
+def scatter(g, T, vw):
+    V = g.vector
+    vw()
+    V.wait_ge(T.sem.wvr, 1)
+    V.tensor_copy(T.wv[:].indirect(T.off[:]), T.vals[:]).then_inc(T.sem.scr, 1)
+
+
+def matmuls(g, T, a, b):
+    PE = g.tensor
+    PE.wait_ge(T.sem.scr, 1)
+    for h in range(8):
+        ins = PE.matmul(T.po[:, a:b], T.sel[:, 14 - 2 * h:142 - 2 * h], T.wv[:, 8 * a + h:8 * b:8], h == 0, h == 7)
+    ins.then_inc(T.sem.mo, 1)
+
+
+def finish(g, T, v, vw, a, b):
+    V = g.vector
+    V.wait_ge(T.sem.mo, 1)
+    v(V.tensor_tensor(T.ot[:, a:b], T.po[:, a:b], T.idn[:, a:b], AluOpType.max))
+    vw()
+    V.tensor_scalar(T.inv[:, a:b], T.ot[:, a:b], float(BASE), None, AluOpType.add).then_inc(T.sem.inr, 1)
+
+
+def helper(g, core, T, topo, me):
+    S, V, PE = T.sem, g.vector, g.tensor
+    ts = V.tensor_scalar
+    v, vw = vector_chain(T, V)
+    rid, pid = topo.addr(me, core)
+    m = helper_mask(core, me, topo)
+    g.iota(T.pcol[:], [[0, 1]], 0, 1).then_inc(S.pc, 1)
+    g.iota(T.spare[:], [[16, 32]], QW, 1).then_inc(S.pc, 1)
+    V.memset(T.ones[:, 0:16], 1.0).then_inc(S.ones, 1)
+    v(V.memset(T.sel[:], 0.0))
+    V.wait_ge(S.ones, 1)
+    V.wait_ge(S.pc, 2)
+    v(ts(T.a30[:], T.pcol[:], 30, None, AluOpType.bitwise_and))
+    vw()
+    v(ts(T.c0[:], T.a30[:], 0.0, None, AluOpType.is_equal),
+      ts(T.c1[:], T.a30[:], 16.0, None, AluOpType.is_equal))
+    vw()
+    ts(T.sel[:, 14:144:16], T.ones[:, 0:9], T.c0[:], None, AluOpType.mult).then_inc(S.sell, 1)
+    ts(T.sel[:, 15:144:16], T.ones[:, 0:9], T.c1[:], None, AluOpType.mult).then_inc(S.sell, 1)
+    g.wait_ge(S.sell, 2)
+    g.remote_dma(T.sel[:], T.sel[:], S.selr, S.ls, pid, rid, m)
+    g.iota(T.lo[:], [[1, 256]], 0, 0, allow_small_or_imprecise_dtypes=True).then_inc(S.lor, 1)
+    g.iota(T.wv[:, WV:QW], [[0, QW - WV]], -NONE // 2, 0, allow_small_or_imprecise_dtypes=True).then_inc(S.wvr, 1)
+    g.iota(T.idb[:, CH:512], [[16, 512 - CH]], 16 * CH - BASE, 0, allow_small_or_imprecise_dtypes=True).then_inc(S.idr, 1)
+    columns(g, T, v, vw)
+    numbers(g, T, v, vw)
+    make_table(g, T, v, vw, CH, 512)
+    V.wait_ge(S.pia, len(bits(topo.mask(me, core))))
+    offsets(g, T, v, vw)
+    scatter(g, T, vw)
+    PE.wait_ge(S.sell, 2)
+    matmuls(g, T, CH, 512)
+    V.wait_ge(S.idl, 1)
+    finish(g, T, v, vw, CH, 512)
+    g.wait_ge(S.inr, 1)
+    g.remote_dma(T.inv[:, CH:512], T.inv[:, CH:512], S.invh, S.ls, pid, rid, m)
+    g.wait_ge(S.ls, 2 * len(bits(m)))
 
 
 def member(g, core, T, topo, cores, rank):
     S = T.sem
     V, A, PE, SY = g.vector, g.scalar, g.tensor, g.sync
+    cp = V.tensor_copy
     p = plan(rank, cores, topo)
+    hlp = helper_of(core, p, topo)
     copy = ActivationFunctionType.Copy
-    n = [0]
-
-    def v(ins):
-        ins.then_inc(S.v, 1)
-        n[0] += 1
-
-    def vw():
-        V.wait_ge(S.v, n[0])
+    v, vw = vector_chain(T, V)
 
     A.dma_start(T.li[0:16, 128:256], T.plc[:]).then_inc(S.ldp, 16)
     SY.dma_start(T.li[0:16, 0:128], T.snd[:]).then_inc(S.lds, 16)
     SY.dma_start(T.xs[:], T.x[:]).then_inc(S.xl, 16)
-    SY.dma_start(T.win[:, 0:GHA], T.gh[:, 0:GHA]).then_inc(S.ghl, 16)
-    SY.wait_ge(S.sent, 1)
-    SY.dma_start(T.win[:, GHA:G], T.gh[:, GHA:G]).then_inc(S.ghl, 16)
+    for k in range(3):
+        if k:
+            SY.wait_ge(S["sent%d" % (k - 1)], 1)
+        SY.dma_start(T.win[:, GHP[k]:GHP[k + 1]], T.gh[:, GHP[k]:GHP[k + 1]]).then_inc(S.ghl, 16)
 
+    g.iota(T.pcol[:], [[0, 1]], 0, 1).then_inc(S.pc, 1)
+    g.iota(T.spare[:], [[16, 32]], QW, 1).then_inc(S.pc, 1)
     g.wait_ge(S.ones, 1)
     g.affine_select(T.rep[0:16, :], T.ones[0:16, :], [[0, 8], [-1, 16]], AluOpType.is_equal, 0.0, 0, 1).then_inc(S.rep, 1)
-    g.iota(T.pcol[:], [[0, 1]], 0, 1).then_inc(S.pc, 1)
-    g.iota(T.spare[:], [[16, 64]], QW, 1).then_inc(S.pc, 1)
-    g.iota(T.vals[:], [[1, CAP]], 0, 0, allow_small_or_imprecise_dtypes=True).then_inc(S.vl, 1)
-    g.wait_ge(S.selz, 1)
-    g.affine_select(T.sel[:], T.sel[:], [[0, 9], [1024, 4], [-16, 4]], AluOpType.not_equal, 1.0, -3 * 1024, 1).then_inc(S.selr, 1)
-    g.wait_ge(S.selr, 1)
-    g.affine_select(T.sel[:], T.sel[:], [[0, 9], [1024, 4], [-16, 4]], AluOpType.not_equal, 1.0, -3 * 1024 - 64, 1).then_inc(S.selr, 1)
-    g.iota(T.idb[:], [[16, 512]], -2 * NONE, 0, allow_small_or_imprecise_dtypes=True).then_inc(S.idr, 1)
+    g.iota(T.lo[:], [[1, 256]], 0, 0, allow_small_or_imprecise_dtypes=True).then_inc(S.lor, 1)
+    g.iota(T.wv[:, WV:QW], [[0, QW - WV]], -NONE // 2, 0, allow_small_or_imprecise_dtypes=True).then_inc(S.wvr, 1)
 
     V.memset(T.ones[0:16, :], 1.0).then_inc(S.ones, 1)
-    V.memset(T.sel[:], 0.0).then_inc(S.selz, 1)
-    v(V.memset(T.wv[:, 0:QW], -float(NONE)))
-    V.wait_ge(S.pc, 2)
-    v(V.tensor_scalar(T.gri[:], T.pcol[:], 4, 3, AluOpType.logical_shift_right, AluOpType.bitwise_and))
-    v(V.tensor_scalar(T.pmi[:], T.pcol[:], 15, None, AluOpType.bitwise_and))
-    vw()
-    v(V.tensor_copy(T.grf[:], T.gri[:]))
-    v(V.tensor_copy(T.pmf[:], T.pmi[:]))
+    columns(g, T, v, vw)
     V.wait_ge(S.ldp, 16)
-    V.tensor_copy(T.lf[0:16, 128:256], T.li[0:16, 128:256]).then_inc(S.lfp, 1)
+    cp(T.lf[0:16, 128:256], T.li[0:16, 128:256]).then_inc(S.lfp, 1)
     V.wait_ge(S.lds, 16)
-    V.tensor_copy(T.lf[0:16, 0:128], T.li[0:16, 0:128]).then_inc(S.lfs, 1)
+    cp(T.lf[0:16, 0:128], T.li[0:16, 0:128]).then_inc(S.lfs, 1)
     PE.wait_ge(S.rep, 1)
     PE.wait_ge(S.lfp, 1)
     PE.matmul(T.plp[:, 0:128], T.rep[0:16, :], T.lf[0:16, 128:256], True, True).then_inc(S.plpr, 1)
     PE.wait_ge(S.lfs, 1)
     PE.matmul(T.pls[:, 0:128], T.rep[0:16, :], T.lf[0:16, 0:128], True, True).then_inc(S.plsr, 1)
     V.wait_ge(S.plpr, 1)
-    v(V.tensor_copy(T.pi[0:64, :], T.plp[0:64, 0:64]))
-    v(V.tensor_copy(T.pi[64:128, :], T.plp[64:128, 64:128]))
-    vw()
-    v(V.tensor_scalar(T.qi[:], T.pi[:], 2, None, AluOpType.logical_shift_right))
-    v(V.tensor_scalar(T.ai[:], T.pi[:], 3, None, AluOpType.bitwise_and))
-    vw()
-    v(V.tensor_tensor(T.ua[:], T.qi[:], T.spare[:], AluOpType.subtract))
-    v(V.tensor_scalar(T.mine[:], T.ai[:], T.grf[:], None, AluOpType.is_equal))
-    vw()
-    v(V.tensor_tensor(T.ub[:], T.ua[:], T.mine[:], AluOpType.mult))
-    vw()
-    v(V.tensor_tensor(T.uc[:], T.ub[:], T.spare[:], AluOpType.add))
-    vw()
-    v(V.tensor_copy(T.off[:], T.uc[:]))
-    vw()
-    A.wait_ge(S.vl, 1)
-    A.activation(T.vals[64:128, :], T.vals[64:128, :], copy, bias=float(CAP)).then_inc(S.vl2, 1)
-    V.wait_ge(S.vl2, 1)
-    V.tensor_copy(T.wv[:, 0:DW].indirect(T.off[:, 0:32]), T.vals[:, 0:512]).then_inc(S.scr, 1)
+    for e in range(4):
+        cp(T.pi[32 * e:32 * e + 32, :], T.plp[32 * e:32 * e + 32, 32 * e:32 * e + 32]).then_inc(S.pir, 1)
+    numbers(g, T, v, vw)
+    V.wait_ge(S.pir, 4)
+    offsets(g, T, v, vw)
     V.wait_ge(S.plsr, 1)
-    V.tensor_copy(T.so[:], T.pls[:, 0:128]).then_inc(S.sor, 1)
-    V.wait_ge(S.selr, 2)
-    V.tensor_copy(T.selh[:], T.sel[:]).then_inc(S.selc, 1)
+    cp(T.so[:], T.pls[:, 0:128]).then_inc(S.sor, 1)
+    scatter(g, T, vw)
+    PE.wait_ge(S.selr, len(bits(helper_mask(hlp, core, topo))))
+    matmuls(g, T, 0, CH)
 
     for q in (V, A):
         q.wait_ge(S.xl, 16)
         q.wait_ge(S.sor, 1)
     for k in (0, 1):
-        a, b, c = k * HALF, k * HALF + HALF, CAP + k * HALF
-        V.tensor_copy(T.sb[:, a:b], T.xs[:].indirect(T.so[:, a // 16:b // 16])).then_inc(S["vg%d" % k], 1)
-        A.activation(T.sb[:, c:c + HALF], T.xs[:].indirect(T.so[:, c // 16:(c + HALF) // 16]), copy,
-                     bias=-0.0).then_inc(S["sg%d" % k], 1)
+        a, b = STEP[k], STEP[k + 1]
+        cp(T.sb[:, a:b], T.xs[:].indirect(T.so[:, a // 16:b // 16])).then_inc(S["vg%d" % k], 1)
+        a, b = CAP + a, CAP + b
+        A.activation(T.sb[:, a:b], T.xs[:].indirect(T.so[:, a // 16:b // 16]), copy, bias=-0.0).then_inc(S["sg%d" % k], 1)
 
+    g.wait_ge(S.pir, 4)
+    rid, pid = topo.addr(hlp, core)
+    m = topo.mask(core, hlp)
+    g.remote_dma(T.pi[:], T.pi[:], S.pia, S.ls, pid, rid, m)
+    left = len(bits(m))
     eng = relay_engines(core, p, topo)
-    left = 0
     for k in (0, 1):
         g.wait_ge(S["vg%d" % k], 1)
         g.wait_ge(S["sg%d" % k], 1)
+        w = STEP[k + 1] - STEP[k]
         trs = []
         for half, dst, at, relays in p:
+            a = half * CAP + STEP[k]
             if relays:
-                c = relays[k]
-                rid, pid = topo.addr(c, core)
-                a = half * CAP + k * HALF
-                trs.append(RemoteDMATransfer(dst_ids=[DstId(rid=rid, pnc=pid)], dma_engine_mask=maskof(eng[c]),
-                                             remote_sem=S.rin, src=T.sb[:, a:a + HALF], dst=T.rb[:]))
-                left += len(eng[c])
-        if trs:
-            g.remote_dma_fused(trs, local_sem=S.ls)
-    for half, dst, at, relays in p:
-        if not relays:
-            rid, pid = topo.addr(dst, core)
-            m = topo.mask(core, dst)
-            g.remote_dma(T.win[:, at:at + CAP], T.sb[:, half * CAP:(half + 1) * CAP], S.arr, S.ls, pid, rid, m)
-            left += len(bits(m))
-    g.sem_inc(S.sent, 1)
+                c, es, sem, land = relays[k], eng[relays[k]], S.rin, T.rb[:, 0:w]
+            else:
+                c, es, sem, land = dst, bits(topo.mask(core, dst)), S.arr, T.win[:, at + STEP[k]:at + STEP[k + 1]]
+            rid, pid = topo.addr(c, core)
+            trs.append(RemoteDMATransfer(dst_ids=[DstId(rid=rid, pnc=pid)], dma_engine_mask=maskof(es), remote_sem=sem,
+                                         src=T.sb[:, a:a + w], dst=land))
+            left += len(es)
+        g.remote_dma_fused(trs, local_sem=S.ls)
+        g.sem_inc(S["sent%d" % k], 1)
     g.wait_ge(S.ls, left)
 
-    V.wait_ge(S.scr, 1)
-    V.tensor_copy(T.wv[:, 0:DW].indirect(T.off[:, 32:64]), T.vals[:, 512:CAP]).then_inc(S.scs, 1)
-    V.wait_ge(S.scs, 1)
-    PE.wait_ge(S.selc, 1)
-    for h in range(4):
-        V.tensor_copy(T.wh[:, 512 * h:512 * h + 512], T.wv[:, h:QW:4]).then_inc(S["cv%d" % h], 1)
-        PE.wait_ge(S["cv%d" % h], 1)
-        ins = PE.matmul(T.po[:], T.selh[:, 12 - 4 * h:140 - 4 * h], T.wh[:, 512 * h:512 * h + 512], h == 0, h == 3)
-    ins.then_inc(S.mo, 1)
-    V.wait_ge(S.idr, 1)
-    v(V.tensor_scalar(T.idn[:], T.idb[:], T.pmf[:], None, AluOpType.add))
-    vw()
-    V.wait_ge(S.mo, 1)
-    v(V.tensor_tensor(T.ot[:], T.po[:], T.idn[:], AluOpType.max))
-    vw()
-    V.tensor_scalar(T.inv[:], T.ot[:], float(2 * NONE), None, AluOpType.add).then_inc(S.inr, 1)
+    V.wait_ge(S.idnr, sum(len(bits(topo.mask(c, dst))) for half, dst, at, relays in p for c in relays))
+    finish(g, T, v, vw, 0, CH)
 
     total = arrivals(rank, cores, topo)
     for q in (V, A):
         q.wait_ge(S.inr, 1)
-        q.wait_ge(S.ghl, 32)
+        q.wait_ge(S.ghl, 48)
         q.wait_ge(S.arr, total)
     at = 0
     for k, w in enumerate(BLOCKS):
         a, b, c = at, at + w, at + 2 * w
-        V.tensor_copy(T.yb[:, a:b], T.win[:].indirect(T.inv[:, a // 16:b // 16])).then_inc(S["yv%d" % k], 1)
+        if k == NB - 1:
+            for q in (V, A):
+                q.wait_ge(S.invh, len(bits(helper_mask(hlp, core, topo))))
+        cp(T.yb[:, a:b], T.win[:].indirect(T.inv[:, a // 16:b // 16])).then_inc(S["yv%d" % k], 1)
         A.activation(T.yb[:, b:c], T.win[:].indirect(T.inv[:, b // 16:c // 16]), copy, bias=-0.0).then_inc(S["ys%d" % k], 1)
         SY.wait_ge(S["yv%d" % k], 1)
-        SY.dma_start(T.y[:, a:b], T.yb[:, a:b]).then_inc(S.st, 16)
         SY.wait_ge(S["ys%d" % k], 1)
-        SY.dma_start(T.y[:, b:c], T.yb[:, b:c]).then_inc(S.st, 16)
+        SY.dma_start(T.y[:, a:c], T.yb[:, a:c]).then_inc(S.st, 16)
         at = c
-    SY.wait_ge(S.st, 2 * NB * 16)
+    SY.wait_ge(S.st, NB * 16)

@@ -6,14 +6,18 @@ G, CAP = 8192, 1024
 STEP = [0, 608, 1024]
 ENT = 2 * CAP // 4
 QW = G // 2
-DW = QW + ENT + 128
+DW = 2 * QW
 WV = 3072
+FV = 512
 NONE = 8192
 BASE = 4 * NONE
-GHP = [0, 3072, 5632, 8192]
-BLOCKS = [384, 704, 1024, 960, 640, 384]
+BLOCKS = [448, 960, 1152, 960, 576]
+PART = [2, 1, 2]
 NB = len(BLOCKS)
-CH = (G - 2 * BLOCKS[-1]) // 16
+EDGE = [G - 2 * sum(BLOCKS[:k]) for k in range(NB + 1)]
+IB = [EDGE[sum(PART[:j])] // 16 for j in range(4)]
+CH = IB[1]
+LOW = EDGE[PART[0]]
 
 COLI = ["pcol", "pm", "gr", "e5", "a30"]
 COLF = ["grf", "pmf", "cs0", "cs1", "c0", "c1", "ef", "be0", "be1"]
@@ -30,13 +34,10 @@ SCRATCH = {
     "ones": ("sbuf", [128, 128], "float32"),
     "rep": ("sbuf", [128, 128], "float32"),
     "sel": ("sbuf", [128, 144], "bfloat16"),
-    "spare": ("sbuf", [128, 32], "int32"),
     "pi": ("sbuf", [128, 32], "int32"),
     "qi": ("sbuf", [128, 32], "int32"),
     "ai": ("sbuf", [128, 32], "int32"),
-    "mine": ("sbuf", [128, 32], "float32"),
     "ua": ("sbuf", [128, 32], "float32"),
-    "ub": ("sbuf", [128, 32], "float32"),
     "uc": ("sbuf", [128, 32], "float32"),
     "off": ("sbuf", [128, 32], "uint16"),
     "lo": ("sbuf", [128, 256], "float32"),
@@ -48,13 +49,16 @@ SCRATCH = {
     "inv": ("sbuf", [128, 512], "uint16"),
     "plp": ("psum", [128, 512], "float32"),
     "pls": ("psum", [128, 512], "float32"),
-    "po": ("psum", [128, 512], "float32"),
+    "po0": ("psum", [128, 512], "float32"),
+    "po1": ("psum", [128, 512], "float32"),
+    "po2": ("psum", [128, 512], "float32"),
 }
 SCRATCH.update({k: ("sbuf", [128, 1], "int32") for k in COLI})
 SCRATCH.update({k: ("sbuf", [128, 1], "float32") for k in COLF})
-SEMAPHORES = ["ldp", "lds", "xl", "ghl", "st", "ones", "v", "rep", "pc", "lor", "wvr", "sell", "selr", "idr", "idl", "idnr", "lfp",
-              "lfs", "plpr", "plsr", "pir", "pia", "sor", "scr", "mo", "inr", "invh", "vg0", "vg1", "sg0", "sg1", "sent0", "sent1",
-              "ls", "rin", "arr"] + ["yv%d" % k for k in range(NB)] + ["ys%d" % k for k in range(NB)]
+SEMAPHORES = ["ldp", "lds", "xl", "gh0", "gh1", "st", "ones", "v", "rep", "pc", "lor", "wvr", "fill", "sell", "selr", "idr", "idl",
+              "idnr", "lfp", "lfs", "plpr", "plsr", "pir", "pia", "sor", "scr", "mo0", "mo1", "mo2", "in0", "in1", "in2", "invh1",
+              "invh2", "vg0", "vg1", "sg0", "sg1", "sent", "ls", "rin", "arr0", "arr1"]
+SEMAPHORES += ["yv%d" % k for k in range(NB)] + ["ys%d" % k for k in range(NB)]
 
 
 def bits(m):
@@ -92,10 +96,6 @@ def helper_of(me, p, topo):
     return [c for c in chip_of(me, topo) if topo.die(c) == topo.die(me) and c not in relays_of(p)][0]
 
 
-def helper_mask(helper, me, topo):
-    return maskof(bits(topo.mask(helper, me))[::2])
-
-
 def relay_engines(me, p, topo):
     taken = []
     for half, dst, at, relays in p:
@@ -112,17 +112,18 @@ def relay_engines(me, p, topo):
 
 
 def arrivals(rank, cores, topo):
-    n, total = len(cores), 0
+    n, total = len(cores), [0, 0]
     for s in ((rank - 1) % n, (rank + 1) % n):
         for half, dst, at, relays in plan(s, cores, topo):
             if dst == cores[rank]:
-                for c in (relays or [cores[s]] * 2):
-                    total += len(bits(topo.mask(c, dst)))
+                for k, c in enumerate(relays or [cores[s]] * 2):
+                    total[k] += len(bits(topo.mask(c, dst)))
     return total
 
 
 def table_part(k, n):
-    return CH * k // n // 4 * 4, CH * (k + 1) // n // 4 * 4
+    w = G // 16 - CH
+    return CH + w * k // n // 4 * 4, CH + w * (k + 1) // n // 4 * 4
 
 
 def rank_program(g, core, T, topo):
@@ -180,15 +181,14 @@ def relay(g, core, T, topo, me, p):
     rid, pid = topo.addr(dst, core)
     k = relays.index(core)
     g.wait_ge(S.rin, len(relay_engines(me, p, topo)[core]))
-    g.remote_dma(T.win[:, at + STEP[k]:at + STEP[k + 1]], T.rb[:, 0:STEP[k + 1] - STEP[k]], S.arr, S.ls, pid, rid, m)
+    g.remote_dma(T.win[:, at + STEP[k]:at + STEP[k + 1]], T.rb[:, 0:STEP[k + 1] - STEP[k]], S["arr%d" % k], S.ls, pid, rid, m)
     g.wait_ge(S.ls, 2 * len(bits(m)))
 
 
 def columns(g, T, v, vw):
     S, V = T.sem, g.vector
     ts = V.tensor_scalar
-    v(V.memset(T.wv[:, 0:WV], -float(NONE // 2)))
-    V.wait_ge(S.pc, 2)
+    V.wait_ge(S.pc, 1)
     v(ts(T.pm[:], T.pcol[:], 15, None, AluOpType.bitwise_and),
       ts(T.e5[:], T.pcol[:], 5, None, AluOpType.logical_shift_right),
       ts(T.gr[:], T.pcol[:], 4, 1, AluOpType.logical_shift_right, AluOpType.bitwise_and))
@@ -198,14 +198,14 @@ def columns(g, T, v, vw):
       ts(T.cs1[:], T.pm[:], 1.0, None, AluOpType.is_equal),
       ts(T.ef[:], T.e5[:], float(ENT), None, AluOpType.mult))
     vw()
+    v(V.tensor_tensor(T.be0[:], T.ef[:], T.cs0[:], AluOpType.mult))
+    vw()
+    v(ts(T.be1[:], T.cs0[:], 256.0, T.be0[:], AluOpType.mult, AluOpType.add))
 
 
 def numbers(g, T, v, vw):
     S, V = T.sem, g.vector
     ts = V.tensor_scalar
-    v(V.tensor_tensor(T.be0[:], T.ef[:], T.cs0[:], AluOpType.mult))
-    vw()
-    v(ts(T.be1[:], T.cs0[:], 256.0, T.be0[:], AluOpType.mult, AluOpType.add))
     vw()
     V.wait_ge(S.lor, 1)
     v(ts(T.vals[:, 0:256], T.lo[:], T.cs1[:], T.be0[:], AluOpType.mult, AluOpType.add),
@@ -218,12 +218,9 @@ def offsets(g, T, v, vw):
     v(ts(T.qi[:], T.pi[:], 1, None, AluOpType.logical_shift_right),
       ts(T.ai[:], T.pi[:], 1, None, AluOpType.bitwise_and))
     vw()
-    v(tt(T.ua[:], T.qi[:], T.spare[:], AluOpType.subtract),
-      ts(T.mine[:], T.ai[:], T.grf[:], None, AluOpType.is_equal))
+    v(ts(T.ua[:], T.ai[:], T.grf[:], float(QW), AluOpType.not_equal, AluOpType.mult))
     vw()
-    v(tt(T.ub[:], T.ua[:], T.mine[:], AluOpType.mult))
-    vw()
-    v(tt(T.uc[:], T.ub[:], T.spare[:], AluOpType.add))
+    v(tt(T.uc[:], T.qi[:], T.ua[:], AluOpType.add))
     vw()
     v(V.tensor_copy(T.off[:], T.uc[:]))
 
@@ -235,20 +232,19 @@ def scatter(g, T, vw):
     V.tensor_copy(T.wv[:].indirect(T.off[:]), T.vals[:]).then_inc(T.sem.scr, 1)
 
 
-def matmuls(g, T, a, b):
-    PE = g.tensor
-    PE.wait_ge(T.sem.scr, 1)
+def matmuls(g, T, j):
+    PE, a, b = g.tensor, IB[j + 1], IB[j]
     for h in range(8):
-        ins = PE.matmul(T.po[:, a:b], T.sel[:, 14 - 2 * h:142 - 2 * h], T.wv[:, 8 * a + h:8 * b:8], h == 0, h == 7)
-    ins.then_inc(T.sem.mo, 1)
+        ins = PE.matmul(T["po%d" % j][:, a:b], T.sel[:, 14 - 2 * h:142 - 2 * h], T.wv[:, 8 * a + h:8 * b:8], h == 0, h == 7)
+    ins.then_inc(T.sem["mo%d" % j], 1)
 
 
-def finish(g, T, v, vw, a, b):
-    V = g.vector
-    V.wait_ge(T.sem.mo, 1)
-    v(V.tensor_tensor(T.ot[:, a:b], T.po[:, a:b], T.idn[:, a:b], AluOpType.max))
+def finish(g, T, v, vw, j, low):
+    V, a, b = g.vector, IB[j + 1], IB[j]
+    V.wait_ge(T.sem["mo%d" % j], 1)
+    v(V.tensor_tensor(T.ot[:, a:b], T["po%d" % j][:, a:b], T.idn[:, a:b], AluOpType.max))
     vw()
-    V.tensor_scalar(T.inv[:, a:b], T.ot[:, a:b], float(BASE), None, AluOpType.add).then_inc(T.sem.inr, 1)
+    V.tensor_scalar(T.inv[:, a:b], T.ot[:, a:b], float(BASE - low), None, AluOpType.add).then_inc(T.sem["in%d" % j], 1)
 
 
 def helper(g, core, T, topo, me):
@@ -256,13 +252,12 @@ def helper(g, core, T, topo, me):
     ts = V.tensor_scalar
     v, vw = vector_chain(T, V)
     rid, pid = topo.addr(me, core)
-    m = helper_mask(core, me, topo)
+    m = topo.mask(core, me)
     g.iota(T.pcol[:], [[0, 1]], 0, 1).then_inc(S.pc, 1)
-    g.iota(T.spare[:], [[16, 32]], QW, 1).then_inc(S.pc, 1)
     V.memset(T.ones[:, 0:16], 1.0).then_inc(S.ones, 1)
     v(V.memset(T.sel[:], 0.0))
     V.wait_ge(S.ones, 1)
-    V.wait_ge(S.pc, 2)
+    V.wait_ge(S.pc, 1)
     v(ts(T.a30[:], T.pcol[:], 30, None, AluOpType.bitwise_and))
     vw()
     v(ts(T.c0[:], T.a30[:], 0.0, None, AluOpType.is_equal),
@@ -274,20 +269,24 @@ def helper(g, core, T, topo, me):
     g.remote_dma(T.sel[:], T.sel[:], S.selr, S.ls, pid, rid, m)
     g.iota(T.lo[:], [[1, 256]], 0, 0, allow_small_or_imprecise_dtypes=True).then_inc(S.lor, 1)
     g.iota(T.wv[:, WV:QW], [[0, QW - WV]], -NONE // 2, 0, allow_small_or_imprecise_dtypes=True).then_inc(S.wvr, 1)
-    g.iota(T.idb[:, CH:512], [[16, 512 - CH]], 16 * CH - BASE, 0, allow_small_or_imprecise_dtypes=True).then_inc(S.idr, 1)
+    g.iota(T.idb[:, 0:CH], [[16, CH]], -BASE, 0, allow_small_or_imprecise_dtypes=True).then_inc(S.idr, 1)
+    v(V.memset(T.wv[:, 0:WV], -float(NONE // 2)))
     columns(g, T, v, vw)
     numbers(g, T, v, vw)
-    make_table(g, T, v, vw, CH, 512)
+    make_table(g, T, v, vw, 0, CH)
     V.wait_ge(S.pia, len(bits(topo.mask(me, core))))
     offsets(g, T, v, vw)
     scatter(g, T, vw)
     PE.wait_ge(S.sell, 2)
-    matmuls(g, T, CH, 512)
+    PE.wait_ge(S.scr, 1)
     V.wait_ge(S.idl, 1)
-    finish(g, T, v, vw, CH, 512)
-    g.wait_ge(S.inr, 1)
-    g.remote_dma(T.inv[:, CH:512], T.inv[:, CH:512], S.invh, S.ls, pid, rid, m)
-    g.wait_ge(S.ls, 2 * len(bits(m)))
+    for j in (1, 2):
+        matmuls(g, T, j)
+        finish(g, T, v, vw, j, 0)
+        part = T.inv[:, IB[j + 1]:IB[j]]
+        g.wait_ge(S["in%d" % j], 1)
+        g.remote_dma(part, part, S["invh%d" % j], S.ls, pid, rid, m)
+    g.wait_ge(S.ls, 3 * len(bits(m)))
 
 
 def member(g, core, T, topo, cores, rank):
@@ -302,40 +301,43 @@ def member(g, core, T, topo, cores, rank):
     A.dma_start(T.li[0:16, 128:256], T.plc[:]).then_inc(S.ldp, 16)
     SY.dma_start(T.li[0:16, 0:128], T.snd[:]).then_inc(S.lds, 16)
     SY.dma_start(T.xs[:], T.x[:]).then_inc(S.xl, 16)
-    for k in range(3):
-        if k:
-            SY.wait_ge(S["sent%d" % (k - 1)], 1)
-        SY.dma_start(T.win[:, GHP[k]:GHP[k + 1]], T.gh[:, GHP[k]:GHP[k + 1]]).then_inc(S.ghl, 16)
+    SY.dma_start(T.win[:, LOW:G], T.gh[:, LOW:G]).then_inc(S.gh0, 16)
+    SY.wait_ge(S.sent, 1)
+    SY.dma_start(T.win[:, 0:LOW], T.gh[:, 0:LOW]).then_inc(S.gh1, 16)
 
     g.iota(T.pcol[:], [[0, 1]], 0, 1).then_inc(S.pc, 1)
-    g.iota(T.spare[:], [[16, 32]], QW, 1).then_inc(S.pc, 1)
     g.wait_ge(S.ones, 1)
     g.affine_select(T.rep[0:16, :], T.ones[0:16, :], [[0, 8], [-1, 16]], AluOpType.is_equal, 0.0, 0, 1).then_inc(S.rep, 1)
     g.iota(T.lo[:], [[1, 256]], 0, 0, allow_small_or_imprecise_dtypes=True).then_inc(S.lor, 1)
     g.iota(T.wv[:, WV:QW], [[0, QW - WV]], -NONE // 2, 0, allow_small_or_imprecise_dtypes=True).then_inc(S.wvr, 1)
 
     V.memset(T.ones[0:16, :], 1.0).then_inc(S.ones, 1)
+    V.memset(T.wv[:, 0:FV], -float(NONE // 2)).then_inc(S.fill, 1)
+    at, fills = FV, 1
+    while at < WV:
+        w = min(at, WV - at, 1024)
+        A.wait_ge(S.fill, fills)
+        A.activation(T.wv[:, at:at + w], T.wv[:, 0:w], copy, bias=0.0).then_inc(S.fill, 1)
+        at, fills = at + w, fills + 1
     columns(g, T, v, vw)
-    V.wait_ge(S.ldp, 16)
-    cp(T.lf[0:16, 128:256], T.li[0:16, 128:256]).then_inc(S.lfp, 1)
+
     V.wait_ge(S.lds, 16)
     cp(T.lf[0:16, 0:128], T.li[0:16, 0:128]).then_inc(S.lfs, 1)
+    V.wait_ge(S.ldp, 16)
+    cp(T.lf[0:16, 128:256], T.li[0:16, 128:256]).then_inc(S.lfp, 1)
     PE.wait_ge(S.rep, 1)
-    PE.wait_ge(S.lfp, 1)
-    PE.matmul(T.plp[:, 0:128], T.rep[0:16, :], T.lf[0:16, 128:256], True, True).then_inc(S.plpr, 1)
     PE.wait_ge(S.lfs, 1)
     PE.matmul(T.pls[:, 0:128], T.rep[0:16, :], T.lf[0:16, 0:128], True, True).then_inc(S.plsr, 1)
+    PE.wait_ge(S.lfp, 1)
+    PE.matmul(T.plp[:, 0:128], T.rep[0:16, :], T.lf[0:16, 128:256], True, True).then_inc(S.plpr, 1)
+    V.wait_ge(S.plsr, 1)
+    cp(T.so[:], T.pls[:, 0:128]).then_inc(S.sor, 1)
     V.wait_ge(S.plpr, 1)
     for e in range(4):
         cp(T.pi[32 * e:32 * e + 32, :], T.plp[32 * e:32 * e + 32, 32 * e:32 * e + 32]).then_inc(S.pir, 1)
-    numbers(g, T, v, vw)
     V.wait_ge(S.pir, 4)
     offsets(g, T, v, vw)
-    V.wait_ge(S.plsr, 1)
-    cp(T.so[:], T.pls[:, 0:128]).then_inc(S.sor, 1)
-    scatter(g, T, vw)
-    PE.wait_ge(S.selr, len(bits(helper_mask(hlp, core, topo))))
-    matmuls(g, T, 0, CH)
+    numbers(g, T, v, vw)
 
     for q in (V, A):
         q.wait_ge(S.xl, 16)
@@ -345,6 +347,12 @@ def member(g, core, T, topo, cores, rank):
         cp(T.sb[:, a:b], T.xs[:].indirect(T.so[:, a // 16:b // 16])).then_inc(S["vg%d" % k], 1)
         a, b = CAP + a, CAP + b
         A.activation(T.sb[:, a:b], T.xs[:].indirect(T.so[:, a // 16:b // 16]), copy, bias=-0.0).then_inc(S["sg%d" % k], 1)
+
+    V.wait_ge(S.fill, fills)
+    scatter(g, T, vw)
+    PE.wait_ge(S.selr, len(bits(topo.mask(hlp, core))))
+    PE.wait_ge(S.scr, 1)
+    matmuls(g, T, 0)
 
     g.wait_ge(S.pir, 4)
     rid, pid = topo.addr(hlp, core)
@@ -362,33 +370,37 @@ def member(g, core, T, topo, cores, rank):
             if relays:
                 c, es, sem, land = relays[k], eng[relays[k]], S.rin, T.rb[:, 0:w]
             else:
-                c, es, sem, land = dst, bits(topo.mask(core, dst)), S.arr, T.win[:, at + STEP[k]:at + STEP[k + 1]]
+                c, es, sem, land = dst, bits(topo.mask(core, dst)), S["arr%d" % k], T.win[:, at + STEP[k]:at + STEP[k + 1]]
             rid, pid = topo.addr(c, core)
             trs.append(RemoteDMATransfer(dst_ids=[DstId(rid=rid, pnc=pid)], dma_engine_mask=maskof(es), remote_sem=sem,
                                          src=T.sb[:, a:a + w], dst=land))
             left += len(es)
         g.remote_dma_fused(trs, local_sem=S.ls)
-        g.sem_inc(S["sent%d" % k], 1)
+    g.sem_inc(S.sent, 1)
     g.wait_ge(S.ls, left)
 
     V.wait_ge(S.idnr, sum(len(bits(topo.mask(c, dst))) for half, dst, at, relays in p for c in relays))
-    finish(g, T, v, vw, 0, CH)
+    finish(g, T, v, vw, 0, LOW)
 
     total = arrivals(rank, cores, topo)
     for q in (V, A):
-        q.wait_ge(S.inr, 1)
-        q.wait_ge(S.ghl, 48)
-        q.wait_ge(S.arr, total)
-    at = 0
-    for k, w in enumerate(BLOCKS):
-        a, b, c = at, at + w, at + 2 * w
-        if k == NB - 1:
-            for q in (V, A):
-                q.wait_ge(S.invh, len(bits(helper_mask(hlp, core, topo))))
-        cp(T.yb[:, a:b], T.win[:].indirect(T.inv[:, a // 16:b // 16])).then_inc(S["yv%d" % k], 1)
-        A.activation(T.yb[:, b:c], T.win[:].indirect(T.inv[:, b // 16:c // 16]), copy, bias=-0.0).then_inc(S["ys%d" % k], 1)
+        for k in (0, 1):
+            q.wait_ge(S["arr%d" % k], total[k])
+    for k in range(NB):
+        a, b, c = EDGE[k + 1], EDGE[k + 1] + BLOCKS[k], EDGE[k]
+        for q in (V, A):
+            if k == 0:
+                q.wait_ge(S.gh0, 16)
+                q.wait_ge(S.in0, 1)
+            if k == PART[0]:
+                q.wait_ge(S.gh1, 16)
+            for j in (1, 2):
+                if k == sum(PART[:j]):
+                    q.wait_ge(S["invh%d" % j], len(bits(topo.mask(hlp, core))))
+        w = T.win[:, LOW if k < PART[0] else 0:G + 2 * CAP]
+        cp(T.yb[:, a:b], w.indirect(T.inv[:, a // 16:b // 16])).then_inc(S["yv%d" % k], 1)
+        A.activation(T.yb[:, b:c], w.indirect(T.inv[:, b // 16:c // 16]), copy, bias=-0.0).then_inc(S["ys%d" % k], 1)
         SY.wait_ge(S["yv%d" % k], 1)
         SY.wait_ge(S["ys%d" % k], 1)
         SY.dma_start(T.y[:, a:c], T.yb[:, a:c]).then_inc(S.st, 16)
-        at = c
     SY.wait_ge(S.st, NB * 16)

from concourse.bass import DstId, RemoteDMATransfer
from concourse.mybir import AluOpType, ActivationFunctionType

ALL = 256
G, CAP = 8192, 1024
STEP = [0, 608, 1024]
ENT = 2 * CAP // 4
QW = G // 2
DW = 2 * QW
WV = 3072
FV = 512
NONE = 8192
BASE = 4 * NONE
BLOCKS = [448, 960, 1152, 960, 576]
PART = [2, 1, 2]
NB = len(BLOCKS)
EDGE = [G - 2 * sum(BLOCKS[:k]) for k in range(NB + 1)]
IB = [EDGE[sum(PART[:j])] // 16 for j in range(4)]
CH = IB[1]
LOW = EDGE[PART[0]]

COLI = ["pcol", "pm", "gr", "e5", "a30"]
COLF = ["grf", "pmf", "cs0", "cs1", "c0", "c1", "ef", "be0", "be1"]

SCRATCH = {
    "xs": ("sbuf", [128, 8192], "bfloat16"),
    "win": ("sbuf", [128, G + 2 * CAP], "bfloat16"),
    "yb": ("sbuf", [128, G], "bfloat16"),
    "sb": ("sbuf", [128, 2 * CAP], "bfloat16"),
    "rb": ("sbuf", [128, STEP[1]], "bfloat16"),
    "li": ("sbuf", [128, 256], "int32"),
    "lf": ("sbuf", [128, 256], "float32"),
    "so": ("sbuf", [128, 128], "uint16"),
    "ones": ("sbuf", [128, 128], "float32"),
    "rep": ("sbuf", [128, 128], "float32"),
    "sel": ("sbuf", [128, 144], "bfloat16"),
    "pi": ("sbuf", [128, 32], "int32"),
    "qi": ("sbuf", [128, 32], "int32"),
    "ai": ("sbuf", [128, 32], "int32"),
    "ua": ("sbuf", [128, 32], "float32"),
    "uc": ("sbuf", [128, 32], "float32"),
    "off": ("sbuf", [128, 32], "uint16"),
    "lo": ("sbuf", [128, 256], "float32"),
    "vals": ("sbuf", [128, ENT], "bfloat16"),
    "wv": ("sbuf", [128, DW], "bfloat16"),
    "idb": ("sbuf", [128, 512], "float32"),
    "idn": ("sbuf", [128, 512], "float32"),
    "ot": ("sbuf", [128, 512], "float32"),
    "inv": ("sbuf", [128, 512], "uint16"),
    "plp": ("psum", [128, 512], "float32"),
    "pls": ("psum", [128, 512], "float32"),
    "po0": ("psum", [128, 512], "float32"),
    "po1": ("psum", [128, 512], "float32"),
    "po2": ("psum", [128, 512], "float32"),
}
SCRATCH.update({k: ("sbuf", [128, 1], "int32") for k in COLI})
SCRATCH.update({k: ("sbuf", [128, 1], "float32") for k in COLF})
SEMAPHORES = ["ldp", "lds", "xl", "gh0", "gh1", "st", "ones", "v", "rep", "pc", "lor", "wvr", "fill", "sell", "selr", "idr", "idl",
              "idnr", "lfp", "lfs", "plpr", "plsr", "pir", "pia", "sor", "scr", "mo0", "mo1", "mo2", "in0", "in1", "in2", "invh1",
              "invh2", "vg0", "vg1", "sg0", "sg1", "sent", "ls", "rin", "arr0", "arr1"]
SEMAPHORES += ["yv%d" % k for k in range(NB)] + ["ys%d" % k for k in range(NB)]


def bits(m):
    return [e for e in range(16) if m >> e & 1]


def maskof(es):
    return sum(1 << e for e in es)


def chip_of(me, topo):
    return [c for c in range(ALL) if topo.host(c) == topo.host(me) and topo.chip(c) == topo.chip(me) and c != me]


def plan(rank, cores, topo):
    n, me = len(cores), cores[rank]
    used, out = [], []
    for half, dst in ((0, cores[(rank - 1) % n]), (1, cores[(rank + 1) % n])):
        relays = []
        if not topo.may_write(me, dst):
            free = [c for c in chip_of(me, topo) if topo.may_write(c, dst) and c not in used]
            near = [c for c in free if topo.die(c) == topo.die(me)]
            far = [c for c in free if topo.die(c) != topo.die(me)]
            relays = [far[0], near[0]] if used else [near[0], far[0]]
            used += relays
        out.append((half, dst, G + (CAP if half == 0 else 0), relays))
    return out


def relays_of(p):
    return [c for half, dst, at, relays in p for c in relays]


def helper_of(me, p, topo):
    return [c for c in chip_of(me, topo) if topo.die(c) == topo.die(me) and c not in relays_of(p)][0]


def relay_engines(me, p, topo):
    taken = []
    for half, dst, at, relays in p:
        if not relays:
            taken += bits(topo.mask(me, dst))
    out = {}
    rel = [relays for half, dst, at, relays in p if relays]
    for step in (0, 1):
        cs = sorted([relays[step] for relays in rel], key=lambda c: topo.die(c) != topo.die(me))
        for k, c in enumerate(cs):
            es = [e for e in bits(topo.mask(me, c)) if e not in taken]
            out[c] = es[k::len(cs)]
    return out


def arrivals(rank, cores, topo):
    n, total = len(cores), [0, 0]
    for s in ((rank - 1) % n, (rank + 1) % n):
        for half, dst, at, relays in plan(s, cores, topo):
            if dst == cores[rank]:
                for k, c in enumerate(relays or [cores[s]] * 2):
                    total[k] += len(bits(topo.mask(c, dst)))
    return total


def table_part(k, n):
    w = G // 16 - CH
    return CH + w * k // n // 4 * 4, CH + w * (k + 1) // n // 4 * 4


def rank_program(g, core, T, topo):
    rank = T.rank_of(core)
    cores = list(T.cores)
    if rank is not None:
        member(g, core, T, topo, cores, rank)
        return
    for r, me in enumerate(cores):
        if core in chip_of(me, topo):
            p = plan(r, cores, topo)
            if core in relays_of(p):
                relay(g, core, T, topo, me, p)
            elif core == helper_of(me, p, topo):
                helper(g, core, T, topo, me)


def vector_chain(T, V):
    n = [0]

    def v(*ins):
        for i in ins:
            i.then_inc(T.sem.v, 1)
            n[0] += 1

    def vw():
        V.wait_ge(T.sem.v, n[0])
    return v, vw


def make_table(g, T, v, vw, a, b):
    V = g.vector
    v(V.tensor_copy(T.pmf[:], T.pm[:]))
    vw()
    V.wait_ge(T.sem.idr, 1)
    V.tensor_scalar(T.idn[:, a:b], T.idb[:, a:b], T.pmf[:], None, AluOpType.add).then_inc(T.sem.idl, 1)


def relay(g, core, T, topo, me, p):
    S, V = T.sem, g.vector
    v, vw = vector_chain(T, V)
    rel = relays_of(p)
    half, dst, at, relays = [q for q in p if core in q[3]][0]
    m = topo.mask(core, dst)
    a, b = table_part(rel.index(core), len(rel))
    g.iota(T.pcol[:], [[0, 1]], 0, 1).then_inc(S.pc, 1)
    g.iota(T.idb[:, a:b], [[16, b - a]], 16 * a - BASE, 0, allow_small_or_imprecise_dtypes=True).then_inc(S.idr, 1)
    V.wait_ge(S.pc, 1)
    v(V.tensor_scalar(T.pm[:], T.pcol[:], 15, None, AluOpType.bitwise_and))
    vw()
    make_table(g, T, v, vw, a, b)
    g.wait_ge(S.idl, 1)
    rid, pid = topo.addr(me, core)
    g.remote_dma(T.idn[:, a:b], T.idn[:, a:b], S.idnr, S.ls, pid, rid, m)
    rid, pid = topo.addr(dst, core)
    k = relays.index(core)
    g.wait_ge(S.rin, len(relay_engines(me, p, topo)[core]))
    g.remote_dma(T.win[:, at + STEP[k]:at + STEP[k + 1]], T.rb[:, 0:STEP[k + 1] - STEP[k]], S["arr%d" % k], S.ls, pid, rid, m)
    g.wait_ge(S.ls, 2 * len(bits(m)))


def columns(g, T, v, vw):
    S, V = T.sem, g.vector
    ts = V.tensor_scalar
    V.wait_ge(S.pc, 1)
    v(ts(T.pm[:], T.pcol[:], 15, None, AluOpType.bitwise_and),
      ts(T.e5[:], T.pcol[:], 5, None, AluOpType.logical_shift_right),
      ts(T.gr[:], T.pcol[:], 4, 1, AluOpType.logical_shift_right, AluOpType.bitwise_and))
    vw()
    v(V.tensor_copy(T.grf[:], T.gr[:]),
      ts(T.cs0[:], T.pm[:], 0.0, None, AluOpType.is_equal),
      ts(T.cs1[:], T.pm[:], 1.0, None, AluOpType.is_equal),
      ts(T.ef[:], T.e5[:], float(ENT), None, AluOpType.mult))
    vw()
    v(V.tensor_tensor(T.be0[:], T.ef[:], T.cs0[:], AluOpType.mult))
    vw()
    v(ts(T.be1[:], T.cs0[:], 256.0, T.be0[:], AluOpType.mult, AluOpType.add))


def numbers(g, T, v, vw):
    S, V = T.sem, g.vector
    ts = V.tensor_scalar
    vw()
    V.wait_ge(S.lor, 1)
    v(ts(T.vals[:, 0:256], T.lo[:], T.cs1[:], T.be0[:], AluOpType.mult, AluOpType.add),
      ts(T.vals[:, 256:512], T.lo[:], T.cs1[:], T.be1[:], AluOpType.mult, AluOpType.add))


def offsets(g, T, v, vw):
    V = g.vector
    ts, tt = V.tensor_scalar, V.tensor_tensor
    v(ts(T.qi[:], T.pi[:], 1, None, AluOpType.logical_shift_right),
      ts(T.ai[:], T.pi[:], 1, None, AluOpType.bitwise_and))
    vw()
    v(ts(T.ua[:], T.ai[:], T.grf[:], float(QW), AluOpType.not_equal, AluOpType.mult))
    vw()
    v(tt(T.uc[:], T.qi[:], T.ua[:], AluOpType.add))
    vw()
    v(V.tensor_copy(T.off[:], T.uc[:]))


def scatter(g, T, vw):
    V = g.vector
    vw()
    V.wait_ge(T.sem.wvr, 1)
    V.tensor_copy(T.wv[:].indirect(T.off[:]), T.vals[:]).then_inc(T.sem.scr, 1)


def matmuls(g, T, j):
    PE, a, b = g.tensor, IB[j + 1], IB[j]
    for h in range(8):
        ins = PE.matmul(T["po%d" % j][:, a:b], T.sel[:, 14 - 2 * h:142 - 2 * h], T.wv[:, 8 * a + h:8 * b:8], h == 0, h == 7)
    ins.then_inc(T.sem["mo%d" % j], 1)


def finish(g, T, v, vw, j, low):
    V, a, b = g.vector, IB[j + 1], IB[j]
    V.wait_ge(T.sem["mo%d" % j], 1)
    v(V.tensor_tensor(T.ot[:, a:b], T["po%d" % j][:, a:b], T.idn[:, a:b], AluOpType.max))
    vw()
    V.tensor_scalar(T.inv[:, a:b], T.ot[:, a:b], float(BASE - low), None, AluOpType.add).then_inc(T.sem["in%d" % j], 1)


def helper(g, core, T, topo, me):
    S, V, PE = T.sem, g.vector, g.tensor
    ts = V.tensor_scalar
    v, vw = vector_chain(T, V)
    rid, pid = topo.addr(me, core)
    m = topo.mask(core, me)
    g.iota(T.pcol[:], [[0, 1]], 0, 1).then_inc(S.pc, 1)
    V.memset(T.ones[:, 0:16], 1.0).then_inc(S.ones, 1)
    v(V.memset(T.sel[:], 0.0))
    V.wait_ge(S.ones, 1)
    V.wait_ge(S.pc, 1)
    v(ts(T.a30[:], T.pcol[:], 30, None, AluOpType.bitwise_and))
    vw()
    v(ts(T.c0[:], T.a30[:], 0.0, None, AluOpType.is_equal),
      ts(T.c1[:], T.a30[:], 16.0, None, AluOpType.is_equal))
    vw()
    ts(T.sel[:, 14:144:16], T.ones[:, 0:9], T.c0[:], None, AluOpType.mult).then_inc(S.sell, 1)
    ts(T.sel[:, 15:144:16], T.ones[:, 0:9], T.c1[:], None, AluOpType.mult).then_inc(S.sell, 1)
    g.wait_ge(S.sell, 2)
    g.remote_dma(T.sel[:], T.sel[:], S.selr, S.ls, pid, rid, m)
    g.iota(T.lo[:], [[1, 256]], 0, 0, allow_small_or_imprecise_dtypes=True).then_inc(S.lor, 1)
    g.iota(T.wv[:, WV:QW], [[0, QW - WV]], -NONE // 2, 0, allow_small_or_imprecise_dtypes=True).then_inc(S.wvr, 1)
    g.iota(T.idb[:, 0:CH], [[16, CH]], -BASE, 0, allow_small_or_imprecise_dtypes=True).then_inc(S.idr, 1)
    v(V.memset(T.wv[:, 0:WV], -float(NONE // 2)))
    columns(g, T, v, vw)
    numbers(g, T, v, vw)
    make_table(g, T, v, vw, 0, CH)
    V.wait_ge(S.pia, len(bits(topo.mask(me, core))))
    offsets(g, T, v, vw)
    scatter(g, T, vw)
    PE.wait_ge(S.sell, 2)
    PE.wait_ge(S.scr, 1)
    V.wait_ge(S.idl, 1)
    for j in (1, 2):
        matmuls(g, T, j)
        finish(g, T, v, vw, j, 0)
        part = T.inv[:, IB[j + 1]:IB[j]]
        g.wait_ge(S["in%d" % j], 1)
        g.remote_dma(part, part, S["invh%d" % j], S.ls, pid, rid, m)
    g.wait_ge(S.ls, 3 * len(bits(m)))


def member(g, core, T, topo, cores, rank):
    S = T.sem
    V, A, PE, SY = g.vector, g.scalar, g.tensor, g.sync
    cp = V.tensor_copy
    p = plan(rank, cores, topo)
    hlp = helper_of(core, p, topo)
    copy = ActivationFunctionType.Copy
    v, vw = vector_chain(T, V)

    A.dma_start(T.li[0:16, 128:256], T.plc[:]).then_inc(S.ldp, 16)
    SY.dma_start(T.li[0:16, 0:128], T.snd[:]).then_inc(S.lds, 16)
    SY.dma_start(T.xs[:], T.x[:]).then_inc(S.xl, 16)
    SY.dma_start(T.win[:, LOW:G], T.gh[:, LOW:G]).then_inc(S.gh0, 16)
    SY.wait_ge(S.sent, 1)
    SY.dma_start(T.win[:, 0:LOW], T.gh[:, 0:LOW]).then_inc(S.gh1, 16)

    g.iota(T.pcol[:], [[0, 1]], 0, 1).then_inc(S.pc, 1)
    g.wait_ge(S.ones, 1)
    g.affine_select(T.rep[0:16, :], T.ones[0:16, :], [[0, 8], [-1, 16]], AluOpType.is_equal, 0.0, 0, 1).then_inc(S.rep, 1)
    g.iota(T.lo[:], [[1, 256]], 0, 0, allow_small_or_imprecise_dtypes=True).then_inc(S.lor, 1)
    g.iota(T.wv[:, WV:QW], [[0, QW - WV]], -NONE // 2, 0, allow_small_or_imprecise_dtypes=True).then_inc(S.wvr, 1)

    V.memset(T.ones[0:16, :], 1.0).then_inc(S.ones, 1)
    V.memset(T.wv[:, 0:FV], -float(NONE // 2)).then_inc(S.fill, 1)
    at, fills = FV, 1
    while at < WV:
        w = min(at, WV - at, 1024)
        A.wait_ge(S.fill, fills)
        A.activation(T.wv[:, at:at + w], T.wv[:, 0:w], copy, bias=0.0).then_inc(S.fill, 1)
        at, fills = at + w, fills + 1
    columns(g, T, v, vw)

    V.wait_ge(S.lds, 16)
    cp(T.lf[0:16, 0:128], T.li[0:16, 0:128]).then_inc(S.lfs, 1)
    V.wait_ge(S.ldp, 16)
    cp(T.lf[0:16, 128:256], T.li[0:16, 128:256]).then_inc(S.lfp, 1)
    PE.wait_ge(S.rep, 1)
    PE.wait_ge(S.lfs, 1)
    PE.matmul(T.pls[:, 0:128], T.rep[0:16, :], T.lf[0:16, 0:128], True, True).then_inc(S.plsr, 1)
    PE.wait_ge(S.lfp, 1)
    PE.matmul(T.plp[:, 0:128], T.rep[0:16, :], T.lf[0:16, 128:256], True, True).then_inc(S.plpr, 1)
    V.wait_ge(S.plsr, 1)
    cp(T.so[:], T.pls[:, 0:128]).then_inc(S.sor, 1)
    V.wait_ge(S.plpr, 1)
    for e in range(4):
        cp(T.pi[32 * e:32 * e + 32, :], T.plp[32 * e:32 * e + 32, 32 * e:32 * e + 32]).then_inc(S.pir, 1)
    V.wait_ge(S.pir, 4)
    offsets(g, T, v, vw)
    numbers(g, T, v, vw)

    for q in (V, A):
        q.wait_ge(S.xl, 16)
        q.wait_ge(S.sor, 1)
    for k in (0, 1):
        a, b = STEP[k], STEP[k + 1]
        cp(T.sb[:, a:b], T.xs[:].indirect(T.so[:, a // 16:b // 16])).then_inc(S["vg%d" % k], 1)
        a, b = CAP + a, CAP + b
        A.activation(T.sb[:, a:b], T.xs[:].indirect(T.so[:, a // 16:b // 16]), copy, bias=-0.0).then_inc(S["sg%d" % k], 1)

    V.wait_ge(S.fill, fills)
    scatter(g, T, vw)
    PE.wait_ge(S.selr, len(bits(topo.mask(hlp, core))))
    PE.wait_ge(S.scr, 1)
    matmuls(g, T, 0)

    g.wait_ge(S.pir, 4)
    rid, pid = topo.addr(hlp, core)
    m = topo.mask(core, hlp)
    g.remote_dma(T.pi[:], T.pi[:], S.pia, S.ls, pid, rid, m)
    left = len(bits(m))
    eng = relay_engines(core, p, topo)
    for k in (0, 1):
        g.wait_ge(S["vg%d" % k], 1)
        g.wait_ge(S["sg%d" % k], 1)
        w = STEP[k + 1] - STEP[k]
        trs = []
        for half, dst, at, relays in p:
            a = half * CAP + STEP[k]
            if relays:
                c, es, sem, land = relays[k], eng[relays[k]], S.rin, T.rb[:, 0:w]
            else:
                c, es, sem, land = dst, bits(topo.mask(core, dst)), S["arr%d" % k], T.win[:, at + STEP[k]:at + STEP[k + 1]]
            rid, pid = topo.addr(c, core)
            trs.append(RemoteDMATransfer(dst_ids=[DstId(rid=rid, pnc=pid)], dma_engine_mask=maskof(es), remote_sem=sem,
                                         src=T.sb[:, a:a + w], dst=land))
            left += len(es)
        g.remote_dma_fused(trs, local_sem=S.ls)
    g.sem_inc(S.sent, 1)
    g.wait_ge(S.ls, left)

    V.wait_ge(S.idnr, sum(len(bits(topo.mask(c, dst))) for half, dst, at, relays in p for c in relays))
    finish(g, T, v, vw, 0, LOW)

    total = arrivals(rank, cores, topo)
    for q in (V, A):
        for k in (0, 1):
            q.wait_ge(S["arr%d" % k], total[k])
    for k in range(NB):
        a, b, c = EDGE[k + 1], EDGE[k + 1] + BLOCKS[k], EDGE[k]
        for q in (V, A):
            if k == 0:
                q.wait_ge(S.gh0, 16)
                q.wait_ge(S.in0, 1)
            if k == PART[0]:
                q.wait_ge(S.gh1, 16)
            for j in (1, 2):
                if k == sum(PART[:j]):
                    q.wait_ge(S["invh%d" % j], len(bits(topo.mask(hlp, core))))
        w = T.win[:, LOW if k < PART[0] else 0:G + 2 * CAP]
        cp(T.yb[:, a:b], w.indirect(T.inv[:, a // 16:b // 16])).then_inc(S["yv%d" % k], 1)
        A.activation(T.yb[:, b:c], w.indirect(T.inv[:, b // 16:c // 16]), copy, bias=-0.0).then_inc(S["ys%d" % k], 1)
        SY.wait_ge(S["yv%d" % k], 1)
        SY.wait_ge(S["ys%d" % k], 1)
        SY.dma_start(T.y[:, a:c], T.yb[:, a:c]).then_inc(S.st, 16)
    SY.wait_ge(S.st, NB * 16)
